import numpy as np, ml_dtypes
CORES = [242,247,114,119]
N = 4
BF = ml_dtypes.bfloat16
NL, W, B, RO, Q = 60, 1920, 112, 8, 2
def parts(rng):
    X = rng.integers(0, 256, (N, 8, 16, W)); L = rng.integers(0, W, (N, 8, 16, W))
    y = (rng.integers(0, 256, (N, 8, 16, B)) * rng.integers(1, 9, (N, 8, 1, B))) >> 3
    return X, L, y, rng.integers(0, NL, (N, 8, B)), rng.integers(0, 4096, (N, 8, B))
def pack(X, L, y, ln, T):
    return {"xw": np.ascontiguousarray(X.reshape(N, 128, W)).astype(np.float32).astype(BF), "il": np.ascontiguousarray(L.reshape(N, 128, W)).astype(np.int32),
            "y0": np.ascontiguousarray(y.reshape(N, 128, B)).astype(np.float32).astype(BF), "ln0": np.ascontiguousarray(ln).astype(np.int32), "tk0": np.ascontiguousarray(T).astype(np.int32)}
def setup_inputs(rng):
    return pack(*parts(rng))
def setup_inputs_spread(rng):
    X = rng.integers(0, 256, (N, 8, 16, W)) >> rng.integers(0, 9, (N, 8, 1, W)); y = rng.integers(0, 256, (N, 8, 16, B)) >> rng.integers(0, 9, (N, 8, 1, B))
    a = np.exp2(rng.integers(-2, 3, (N, 8, 16, 1))); b = np.exp2(rng.integers(-2, 3, (N, 8, 16, 1)))
    line = np.minimum((NL * rng.random((N, 8, 16, W)) ** a).astype(np.int64), NL - 1); wait = np.minimum((32 * rng.random((N, 8, 16, W)) ** b).astype(np.int64), 31)
    ln = np.minimum((NL * rng.random((N, 8, B)) ** 3).astype(np.int64), NL - 1); T = np.minimum(np.exp2(12 * rng.random((N, 8, B))).astype(np.int64) - 1, 4095)
    return pack(X, 32 * line + wait, y, ln, T)
def ends(rng, top, *shape):
    k = rng.integers(0, 4, shape[:-2] + (1, shape[-1]))
    return top * np.where(k < 2, k, rng.integers(0, 2, shape))
def setup_inputs_ends(rng):
    X = ends(rng, 255, N, 8, 16, W); y = ends(rng, 255, N, 8, 16, B)
    L = np.where(rng.random((N, 8, 16, W)) < 0.8, ends(rng, W - 1, N, 8, 16, W), rng.integers(0, W, (N, 8, 16, W)))
    ln = (NL - 1) * rng.integers(0, 2, (N, 8, B)); T = 4095 * rng.integers(0, 2, (N, 8, B))
    L[..., 0] = 0; L[:, :, 1, 0] = W - 1; L[..., 31] = (W - 1) * rng.integers(0, 2, (N, 8, 16))
    L[..., W - 32] = W - 1; L[:, :, 0, W - 32] = 0; L[..., W - 1] = W - 1; L[:, :, 0, W - 1] = 0
    X[..., 0] = 0; X[..., W - 1] = 0; X[..., W - 2] = 255
    for q in range(N):
        if q == 1:
            for c in (0, 31, W - 2, W - 1): X[q, :, :, c] = 255
            y[q] = np.where(np.argsort(rng.random((8, 16, B)), axis=1) < rng.integers(0, 9, (8, 1, B)), 0, 255)
        else:
            if q == N - 1: y[q] = 0
            for i, l, t, v in ((0, NL - 1, 4095, 0), (B - 1, NL - 1, 4095, 0), (B - 2, NL - 1, 4095, 255), (1, NL - 1, 0, 255), (B - 4, NL - 1, 0, 255), (3, 0, 0, 0), (B - 3, 0, 0, 0)):
                ln[q, :, i] = l; T[q, :, i] = t; y[q, :, :, i] = v
            if q == N - 1: y[q, :7, :, B - 2] = 0
            if q == 2: y[q] = np.where(np.argsort(rng.random((8, 16, B)), axis=1) < rng.integers(9, 17, (8, 1, B)), 0, 255)
    return pack(X, L, y, ln, T)
def setup_inputs_corners(rng):
    X, L, y, ln, T = parts(rng)
    T = np.where(rng.random(T.shape) < 0.7, rng.choice(np.array([0, 15, 16, 31, 32, 4064, 4080, 4095]), T.shape), T)
    ln = np.where(rng.random(ln.shape) < 0.4, rng.choice(np.array([0, NL - 1]), ln.shape), ln)
    for q in range(N):
        for g in range(8):
            e = (q + g) % 8
            if e == 0: ln[q, g] = ln[q, g, 0]; T[q, g] = T[q, g, B - 1]
            elif e == 1: L[q, g] = np.arange(W)
            elif e == 2: L[q, g] = 0
            elif e == 3: L[q, g] = W - 1
            elif e == 4: X[q, g] = np.maximum(X[q, g], 1); y[q, g] = np.where(np.argsort(rng.random((16, B)), axis=0) < rng.integers(8, 10, (1, B)), 0, 255)
            elif e == 5: X[q, g] = 0
            elif e == 6: X[q, g] = 255; y[q, g] = rng.integers(128, 256, (16, B))
            else:
                a = rng.permutation(W)[:B]; ln[q, g] = a >> 5; T[q, g] = (a & 31) + 32 * rng.integers(0, 128, B); h = B // 4
                pl = np.concatenate([np.array([0, W - 1]), 1 + rng.permutation(W - 2)])
                d = rng.permutation(np.concatenate([pl[:h], pl[:h], pl[h:B - h]]))
                L[q, g, 15, a] = (d & 4064) + ((d - T[q, g]) & 31)
    return pack(X, L, y, ln, T)
def setup_inputs_crowd(rng):
    X, L, y, ln, T = parts(rng)
    few = rng.integers(0, NL, (N, 8, 1, 4)); few[:, ::2, :, 0] = NL - 1; few[:, 1::2, :, 1] = 0
    L[:, :, 0:2] = (L[:, :, 0:2] & 31) + 32 * np.take_along_axis(few, rng.integers(0, 4, (N, 8, 1, 2 * W)), 3).reshape(N, 8, 2, W)
    L[:, :, 15:16] = (L[:, :, 15:16] & 31) + 32 * np.take_along_axis(few, rng.integers(0, 2, (N, 8, 1, W)), 3)
    ln = np.take_along_axis(few, rng.integers(0, 4, (N, 8, 1, B)), 3).reshape(N, 8, B)
    p = int(rng.integers(0, N)); q = (p + 1) % N
    X[p] = 0; y[p] = 255 - (rng.integers(0, 128, (8, 16, B)) >> (3 * rng.integers(0, 2, (8, 1, B))))
    X[q] = np.maximum(X[q], 1); y[q] = rng.integers(128, 256, (8, 16, B))
    y[q, int(rng.integers(0, 8)), :, rng.permutation(B)[:int(rng.integers(1, 32))]] = 0
    return pack(X, L, y, ln, T)
def check_inputs(d):
    bad = []
    for k, hi in (("xw", 255), ("il", W - 1), ("y0", 255), ("ln0", NL - 1), ("tk0", 4095)):
        v = np.asarray(d[k]).astype(np.float64)
        if not np.all((v >= 0) & (v <= hi)): bad.append("range of " + k)
        elif not np.all(v == np.floor(v)): bad.append("whole numbers of " + k)
    return bad
def reference(xw, il, y0, ln0, tk0):
    X = xw.astype(np.float32).astype(np.int64).reshape(N, 8, 16, W); L = il.astype(np.int64).reshape(N, 8, 16, W)
    y = y0.astype(np.float32).astype(np.int64).reshape(N, 8, 16, B); ln = ln0.astype(np.int64); T = tk0.astype(np.int64)
    A = np.zeros(N, np.int64)
    for step in range(RO):
        a = 32 * ln + (T & 31)
        c = np.take_along_axis(L, a[:, :, None, :], 3)
        s = (c & 4064) + ((c + T[:, :, None, :]) & 31)
        v = np.take_along_axis(X, np.ascontiguousarray(s.transpose(0, 1, 3, 2)).reshape(N, 8, 1, 16 * B), 3).reshape(N, 8, 16, B, 16 // Q, Q)
        m = np.max(np.min(v, axis=-1), axis=-1)
        z = np.abs(m - y)
        skip = np.add.reduce((z >= y).astype(np.int64), axis=2) >= 9
        ln = np.where(skip, c[:, :, 1], c[:, :, 0]) >> 5
        d = s[:, :, 15]
        T = (T + 1 + (np.add.reduce(z, axis=2) & 31) + (A & 31)[:, None, None]) & 4095
        A = np.add.reduce(skip.reshape(N, 8 * B).astype(np.int64), axis=1)
        y = np.roll(z, 1, axis=0); ln = np.roll(ln, 1, axis=0); T = np.roll(T, 1, axis=0); d = np.roll(d, 1, axis=0)
        for q in range(N):
            for g in range(8):
                p, first = np.unique(d[q, g], return_index=True)
                u = L[q, g]; o = u[:, p]
                u[:, p] = (o & 4064) + ((o + y[q, g][:, first]) & 31)
        if step < RO - 1:
            np.put_along_axis(X, (16 * np.arange(B) + (T & 15))[:, :, None, :], y, 3)
    return {"yw": (L & 31).reshape(N, 128, W).astype(np.float32).astype(BF), "yy": y.reshape(N, 128, B).astype(np.float32).astype(BF), "yl": ln.astype(np.float32), "yt": T.astype(np.float32)}

@@ -1,0 +1,429 @@
+from concourse.mybir import AluOpType as Op, ActivationFunctionType as Act
+
+NR, B, W, STEPS = 4, 112, 1920, 8
+BIG = float(3 * 2 ** 21)
+MAGIC = float(3 * 2 ** 27)
+NV, N1 = 34, 58
+WT = W + B
+
+SCRATCH = {}
+for _names, _w, _t in (
+        ("xt lt", W, "bfloat16"), ("wt", WT, "bfloat16"), ("ili", W, "int32"), ("lf lg", W, "float32"),
+        ("tki lni ci cl ui u5 rz ry ft fu", B, "int32"),
+        ("t0f l0f mk1 qw uf fs fd fl fy fv", B, "float32"),
+        ("mkb iob wdm ge ge2 jk ug wf", B, "bfloat16"), ("so", B, "uint16"),
+        ("ip im pg mg p15 m15", 128, "int32"), ("idf onf s15 e8f on32", 128, "float32"),
+        ("idb nid gb gs se0 se1 nse onb", 128, "bfloat16"),
+        ("g8", 8, "bfloat16"), ("q16 ai aj", 8, "int32"), ("iw c1 cwn nb lose tp8 mn dl sk sd av", 8, "float32"), ("doff", 8, "uint16"),
+        ("acc af1 af2 q25", 1, "float32"), ("af", 4, "float32"),
+        ("qi tq", 16, "int32"), ("lbx ta", 16, "float32"), ("offs", 16, "uint16"),
+        ("r3 w3", 3 * B, "float32"), ("rd eq em", 7 * B, "bfloat16"),
+        ("rp", 16 * N1, "bfloat16"), ("r8", 8 * N1, "bfloat16"), ("vb pm", 16 * B, "bfloat16"), ("mx", 8 * B, "bfloat16"),
+        ("sall", 64, "float32"), ("si sj", 64, "int32"), ("pp pt tpa", 32, "float32"),
+        ("yb", 9 * 336, "bfloat16"),
+        ("ey", 8 * 336, "bfloat16"),
+        ("zo", 8 * B, "bfloat16"), ("eo es", 8 * B, "float32")):
+    for _n in _names.split():
+        SCRATCH[_n] = ("sbuf", [128, _w], _t)
+PSUM = ["b%d" % i for i in range(8)]
+for _n in PSUM:
+    SCRATCH[_n] = ("psum", [128, 512], "float32")
+SEMAPHORES = ["sV", "sS", "sP", "sG", "lsem", "tp1", "tp2", "tp3"] + ["%s%d" % (a, i) for a in ("zr", "ea", "eb") for i in range(8)] + ["d%d" % i for i in range(16)]
+
+
+def rank_program(g, core, T, topo):
+    rank = T.rank_of(core)
+    if rank is None:
+        return
+    cores = T.cores
+    nxt, prv = cores[(rank + 1) % NR], cores[(rank - 1) % NR]
+    V, S, P = g.vector, g.scalar, g.tensor
+    queues = {"V": V, "S": S, "P": P, "G": g, "Y": g.sync}
+    sems = {"V": "sV", "S": "sS", "P": "sP", "G": "sG"}
+    cnt = {"V": 0, "S": 0, "P": 0, "G": 0}
+    know = {q: {} for q in queues}
+    clocks = {}
+    log = {}
+
+    def ensure(q, need):
+        need = {x: i for x, i in need.items() if know[q].get(x, 0) < i}
+        for x in list(need):
+            if any(y != x and clocks.get((y, j), {}).get(x, 0) >= need[x] for y, j in need.items()):
+                del need[x]
+        for x, i in need.items():
+            queues[q].wait_ge(T.sem[sems.get(x, x)], i)
+            for y, j in clocks.get((x, i), {}).items():
+                know[q][y] = max(know[q].get(y, 0), j)
+            know[q][x] = max(know[q].get(x, 0), i)
+
+    def deps(q, reads, writes):
+        need = {}
+        for regs, wr in ((reads, False), (writes, True)):
+            for name, a, b in regs:
+                ps = name in PSUM
+                for (c, d, x, i, w) in log.get(name, []):
+                    if x == q:
+                        if not (w and q != "P" and c < b and a < d):
+                            continue
+                    elif not (ps or (c < b and a < d and (w or wr))):
+                        continue
+                    need[x] = max(need.get(x, 0), i)
+        return need
+
+    def note(x, i, reads, writes):
+        for name, a, b in writes:
+            log[name] = [e for e in log.get(name, []) if not (a <= e[0] and e[1] <= b)] + [(a, b, x, i, True)]
+        for name, a, b in reads:
+            log[name] = [e for e in log.get(name, []) if e[4] or e[2] != x or not (a <= e[0] and e[1] <= b)] + [(a, b, x, i, False)]
+
+    def emit(q, reads, writes, fn):
+        ensure(q, deps(q, reads, writes))
+        fn().then_inc(T.sem[sems[q]], 1)
+        cnt[q] += 1
+        c = dict(know[q])
+        c[q] = cnt[q]
+        clocks[(q, cnt[q])] = c
+        note(q, cnt[q], reads, writes)
+
+    def R(name, a=0, b=None, st=1, p=None):
+        if b is None:
+            b = SCRATCH[name][1][1]
+        t = T[name]
+        if p is None:
+            ap = t[:, a:b] if st == 1 else t[:, a:b:st]
+        else:
+            ap = t[0:p, a:b] if st == 1 else t[0:p, a:b:st]
+        return (ap, [(name, a, b)], [])
+
+    def IND(win, off):
+        return (win[0].indirect(off[0]), win[1], off[1])
+
+    def rd(*ops):
+        return [r for o in ops if isinstance(o, tuple) for r in o[1] + o[2]]
+
+    def ap(o):
+        return o[0] if isinstance(o, tuple) else o
+
+    def tt(out, a, b, op):
+        emit("V", rd(a, b) + out[2], out[1], lambda: V.tensor_tensor(out=out[0], in0=a[0], in1=b[0], op=op))
+
+    def ts(out, a, s1, op0, s2=None, op1=None):
+        if op1 is None:
+            emit("V", rd(a, s1) + out[2], out[1], lambda: V.tensor_scalar(out=out[0], in0=a[0], scalar1=ap(s1), scalar2=None, op0=op0))
+        else:
+            emit("V", rd(a, s1, s2) + out[2], out[1], lambda: V.tensor_scalar(out=out[0], in0=a[0], scalar1=ap(s1), scalar2=ap(s2), op0=op0, op1=op1))
+
+    def cp(out, a):
+        emit("V", rd(a) + out[2], out[1], lambda: V.tensor_copy(out=out[0], in_=a[0]))
+
+    def scan(out, d0, d1, init, op0, op1):
+        emit("V", rd(d0, d1), out[1], lambda: V.tensor_tensor_scan(out=out[0], data0=d0[0], data1=d1[0], initial=init, op0=op0, op1=op1))
+
+    def fill(out, v):
+        emit("V", [], out[1], lambda: V.memset(out[0], v))
+
+    def act(out, a, f, bias=None, acc=None, scale=None):
+        kw = {}
+        if scale is not None:
+            kw["scale"] = scale
+        if bias is not None:
+            kw["bias"] = ap(bias)
+        if acc is not None:
+            kw["accum_out"] = acc[0]
+        emit("S", rd(a, bias), out[1] + (acc[1] if acc is not None else []),
+             lambda: S.activation(out=out[0], in_=a[0], func=f, **kw))
+
+    def mm(out, l, r, start, stop):
+        emit("P", rd(l, r), out[1], lambda: P.matmul(out[0], l[0], r[0], start, stop))
+
+    dma_all = []
+
+    def dma(q, out, src, reads, writes):
+        name = "d%d" % len(dma_all)
+        ensure(q, deps(q, reads, writes))
+        queues[q].dma_start(out=out, in_=src).then_inc(T.sem[name], 16)
+        c = dict(know[q])
+        c[name] = 16
+        clocks[(name, 16)] = c
+        note(name, 16, reads, writes)
+        dma_all.append(name)
+
+    sent = [0]
+
+    def send(dst, out, src, sem):
+        ensure("G", deps("G", src[1], []))
+        rid, pid = topo.addr(dst, core)
+        m = topo.mask(core, dst)
+        g.remote_dma(out_ap=out[0], in_ap=src[0], remote_sem=T.sem[sem], local_sem=T.sem.lsem, pid=pid, routing_id=rid, dma_engine_mask=m)
+        sent[0] += len(topo.engines(core, dst))
+
+    def landed(sem, src, regs):
+        note(sem, len(topo.engines(src, core)), [], regs)
+
+    dma("Y", T.tki[0:8, :], T.tk0[:, :], [], [("tki", 0, B)])
+    dma("S", T.lni[0:8, :], T.ln0[:, :], [], [("lni", 0, B)])
+    C4 = W // 4
+    for j in range(4):
+        dma("YS"[j % 2], T.ili[:, j * C4:(j + 1) * C4], T.il[:, j * C4:(j + 1) * C4], [], [("ili", j * C4, (j + 1) * C4)])
+    dma("S", T.xt[:, :], T.xw[:, :], [], [("xt", 0, W)])
+    dma("Y", T.yb[:, 0:B], T.y0[:, :], [], [("yb", 0, B)])
+
+    def iota(out, pat, base, cm, flag=False):
+        if flag:
+            emit("G", [], out[1], lambda: g.iota(out[0], pat, base, cm, allow_small_or_imprecise_dtypes=True))
+        else:
+            emit("G", [], out[1], lambda: g.iota(out[0], pat, base, cm))
+
+    def pick(out, ones, base):
+        emit("G", ones[1], out[1], lambda: g.affine_select(out=out[0], in_=ones[0], pattern=[[-16, 8], [0, 16]], compare_op=Op.is_equal,
+                                                           fill=0.0, base=base, channel_multiplier=1))
+    iota(R("ip"), [[0, 128]], 0, 1)
+    iota(R("im"), [[1, 128]], 0, 0)
+    fill(R("onb"), 1.0)
+    fill(R("r3"), float(2 ** 24))
+    fill(R("r3", 0, 3 * B, 16), 0.0)
+    iota(R("rp"), [[0, 8 * N1], [-255, 2]], 255, 0, True)
+    pick(R("se0"), R("onb"), 0)
+    pick(R("se1"), R("onb"), -1)
+    fill(R("onf"), 256.0)
+    pick(R("s15"), R("onf"), -15)
+    tt(R("idb"), R("ip"), R("im"), Op.is_equal)
+    ts(R("mg"), R("im"), 4, Op.arith_shift_right)
+    ts(R("p15"), R("ip"), 15, Op.bitwise_and)
+    ts(R("m15"), R("im"), 15, Op.bitwise_and)
+    tt(R("e8f", p=8), R("ip", p=8), R("mg", p=8), Op.is_equal)
+    tt(R("mk1"), R("p15", 0, B), R("m15", 0, B), Op.is_equal)
+    cp(R("t0f", p=8), R("tki", p=8))
+    ts(R("l0f", p=8), R("lni", p=8), 32.0, Op.mult)
+    act(R("mkb"), R("mk1"), Act.Copy, scale=BIG)
+    act(R("nid"), R("idb"), Act.Copy, scale=-1.0)
+    act(R("idf"), R("idb"), Act.Copy)
+    act(R("nse"), R("se0"), Act.Copy, scale=-1.0)
+    P1, PQ, PZ, PL, PK, PW, P6, P7 = PSUM
+    E8 = R("e8f", p=8)
+    mm(R(P1, 0, B), E8, R("t0f", p=8), True, True)
+    mm(R(PQ, 0, B), R("idb"), R("mkb"), True, False)
+    mm(R(PQ, 0, B), E8, R("t0f", p=8), False, True)
+    mm(R(PW, B, 2 * B), R("idb"), R("mkb"), True, False)
+    mm(R(PW, B, 2 * B), E8, R("l0f", p=8), False, True)
+    fill(R("av"), 1.0)
+    fill(R("r8"), 255.0)
+    fill(R("r8", 0, 8 * N1, 8), 0.0)
+    fill(R("tq"), 0)
+    fill(R("lbx"), BIG)
+    ts(R("pg"), R("ip"), 4, Op.arith_shift_right)
+    tt(R("gb"), R("pg"), R("mg"), Op.is_equal)
+    act(R("gs"), R("gb"), Act.Copy, scale=float(2 ** 17))
+    fill(R("rd"), 0.0)
+    fill(R("rd", 0, 784, 112), 4096.0)
+    fill(R("eq"), 4096.0)
+    ts(R("q16"), R("im", 0, 8), 16, Op.mult)
+    tt(R("iw"), R("q16"), R("p15", 0, 8), Op.add)
+
+    def lines_of(j):
+        a, b = j * C4, (j + 1) * C4
+        ts(R("lf", a, b), R("ili", a, b), -15.5, Op.add)
+        act(R("lg", a, b), R("lf", a, b), Act.Identity, MAGIC)
+        act(R("lt", a, b), R("lg", a, b), Act.Identity, -MAGIC)
+
+    def waits_of(j):
+        a, b = j * C4, (j + 1) * C4
+        bank = (PL, PW, PZ, PK)[j]
+        mm(R(bank, 0, C4), R("idb"), R("lt", a, b), True, True)
+        tt(R("wt", a, b), R("ili", a, b), R(bank, 0, C4), Op.subtract)
+    for j in range(3):
+        lines_of(j)
+
+    SEG = lambda name, k=0: R(name, k * B + 15, (k + 1) * B, 16)
+    S7 = lambda name: R(name, 0, 7)
+    NS = NV + N1
+
+    for n in range(STEPS + 1):
+        last = n == STEPS
+        y0 = 336 * n
+        z, lns, clk = R("yb", y0, y0 + B), R("yb", y0 + B, y0 + 2 * B), R("yb", y0 + 2 * B, y0 + 3 * B)
+        if n > 0:
+            k = n - 1
+            e0 = 336 * k
+            ey, el, ec = R("ey", e0, e0 + B), R("ey", e0 + B, e0 + 2 * B), R("ey", e0 + 2 * B, e0 + 3 * B)
+            es = R("es", B * k, B * k + B)
+            landed("ea%d" % k, prv, [("ey", e0, e0 + (336 if k < 7 else 224))])
+            landed("eb%d" % k, prv, es[1])
+            KM = R(P6, 256, 256 + B)
+            mm(KM, R("idb"), R("mkb"), True, False)
+            mm(KM, R("idb"), R("iob"), False, False)
+            mm(KM, R("s15"), es, False, True)
+            mm(R(PK, 0, B), R("idb"), R("iob"), True, False)
+            mm(R(PK, 0, B), R("s15"), es, False, True)
+            for c in (0, B):
+                mm(R(PW, c, c + B), R("idb"), R("mkb"), True, False)
+                if c:
+                    mm(R(PW, c, c + B), R("se1"), el, False, False)
+                mm(R(PW, c, c + B), R("nse" if c else "se0"), el, False, True)
+            mm(R(PZ, 0, B), R("nid"), ey, True, False)
+            if not last:
+                mm(R(PQ, 0, B), R("idb"), R("mkb"), True, False)
+                mm(R(PQ, 0, B), R("idb"), ec, False, False)
+                mm(R(P1, 0, B), R("idb"), ec, True, False)
+            scan(R("w3", 0, B), R("r3", 0, B), KM, 0.0, Op.min, Op.max)
+            tt(S7("nb"), S7("c1"), SEG("w3"), Op.subtract)
+            for q in range(7):
+                L = 16 * q + 16
+                act(R("eq", 112 * q + 112 - L, 112 * q + 112), R(PK, 0, L), Act.Abs, R("nb", q, q + 1))
+            scan(R("w3", B, 3 * B), R("r3", B, 3 * B), R(PW, 0, 2 * B), 0.0, Op.min, Op.max)
+            scan(R("em", 0, 448), R("rd", 0, 448), R("eq", 0, 448), 4096.0, Op.max, Op.min)
+            ts(S7("dl"), SEG("w3", 2), -BIG, Op.add)
+            cp(S7("lbx"), SEG("w3", 1))
+            scan(R("em", 448, 784), R("rd", 448, 784), R("eq", 448, 784), 4096.0, Op.max, Op.min)
+            tt(S7("lose"), R("em", 111, 784, 112), S7("iw"), Op.is_lt)
+            tt(S7("tp8"), S7("lose"), S7("cwn"), Op.mult)
+            tt(S7("mn"), S7("nb"), S7("tp8"), Op.min)
+            ts(S7("doff"), S7("mn"), -1.0 / 256, Op.mult)
+            ts(R("wdm"), IND(R("wt"), S7("doff")), -32.0, Op.add)
+            if last:
+                mm(R(P6, 0, B), R("se0"), el, True, True)
+                mm(R(P6, B, 2 * B), R("se1"), el, True, False)
+                mm(R(P6, B, 2 * B), R("nse"), el, False, True)
+            landed("zr%d" % k, prv, z[1])
+            mm(R(PZ, 0, B), R("idb"), z, False, True)
+            if not last:
+                mm(R(PQ, 0, B), R("gb"), z, False, False)
+                mm(R(P1, 0, B), R("gb"), z, False, True)
+                tt(IND(R("wt"), S7("doff")), R("wdm"), z, Op.add)
+            act(R("ge"), R(PZ, 0, B), Act.Sign, 0.5)
+            mm(R(PQ, 0, B), R("gb" if last else "gs"), R("ge"), last, True)
+        if last:
+            break
+        scan(R("qw"), R("r3", 0, B), R(PQ, 0, B), 0.0, Op.min, Op.max)
+        if n == 0:
+            scan(R("w3", B, 2 * B), R("r3", B, 2 * B), R(PW, B, 2 * B), 0.0, Op.min, Op.max)
+            cp(S7("lbx"), SEG("w3", 1))
+        cp(S7("qi"), SEG("qw"))
+        if n > 0:
+            ts(S7("sk"), SEG("qw"), BIG + 2.0 ** 17, Op.is_ge)
+        ts(S7("tq"), S7("qi"), 31, Op.bitwise_and)
+        if n > 0:
+            ts(R("tq", 8, 15), S7("qi"), 15, Op.bitwise_and)
+            tt(S7("sd"), S7("sk"), S7("dl"), Op.mult)
+        E = 15 if n > 0 else 7
+        tt(R("ta", 0, E), R("tq", 0, E), R("lbx", 0, E), Op.add)
+        if n > 0:
+            tt(S7("ta"), S7("ta"), S7("sd"), Op.add)
+        ts(R("offs", 0, E), R("ta", 0, E), -BIG, Op.add)
+        if n < 7:
+            act(R("uf"), R(P1, 0, B), Act.Identity, MAGIC)
+            act(R("ug"), R("uf"), Act.Identity, -MAGIC)
+            UC = R(P7, 280, 280 + B)
+            if n > 0:
+                mm(UC, R("idb"), ec, True, False)
+                mm(UC, R("gb"), z, False, False)
+            else:
+                mm(UC, E8, R("t0f", p=8), True, False)
+            mm(UC, R("nid"), R("ug"), False, True)
+            act(clk, UC, Act.Identity, R("av", n, n + 1))
+        so = R("eo", B * n, B * n + B)
+        if n > 0:
+            act(R("wf"), IND(R("wt"), S7("offs")), Act.Copy)
+            act(lns, IND(R("lt"), S7("offs")), Act.Copy)
+            cp(IND(R("xt"), R("offs", 8, 15)), z)
+            mm(R(PL, 0, B), R("idb"), lns, True, True)
+            tt(R("ui"), R("wf"), R(P1, 0, B), Op.add)
+            ts(R("u5"), R("ui"), 31, Op.bitwise_and)
+            tt(so, R("u5"), R(PL, 0, B), Op.add)
+        else:
+            cp(R("ci"), IND(R("ili"), S7("offs")))
+            tt(R("ui"), R("ci"), R(P1, 0, B), Op.add)
+            ts(R("cl"), R("ci"), 4064, Op.bitwise_and)
+            ts(R("u5"), R("ui"), 31, Op.bitwise_and)
+            tt(so, R("u5"), R("cl"), Op.add)
+        cp(R("so"), so)
+        if n == 0:
+            cp(lns, R("cl"))
+        send(nxt, R("es", B * n, B * n + B), so, "eb%d" % n)
+        ew = 336 if n < 7 else 224
+        send(nxt, R("ey", y0, y0 + ew), R("yb", y0, y0 + ew), "ea%d" % n)
+        act(R("vb", 16 * NV, 16 * NS), IND(R("xt"), R("so", NV, NS)), Act.Copy)
+        act(R("vb", 16 * NS, 16 * B), IND(R("xt"), R("so", NS, B)), Act.Copy)
+        cp(R("vb", 0, 16 * NV), IND(R("xt"), R("so", 0, NV)))
+        mm(R(PK, 0, NS), R("nid"), R("yb", y0, y0 + NS), True, False)
+        mm(R(P6, 0, B - NS), R("nid"), R("yb", y0 + NS, y0 + B), True, False)
+        for a, b in ((0, NV), (NV, NS), (NS, B)):
+            w = b - a
+            scan(R("pm", 16 * a, 16 * b), R("rp", 0, 16 * w), R("vb", 16 * a, 16 * b), 255.0, Op.max, Op.min)
+            scan(R("mx", 8 * a, 8 * b), R("r8", 0, 8 * w), R("pm", 16 * a + 1, 16 * b, 2), 0.0, Op.min, Op.max)
+        zo = B * n
+        mm(R(PK, 0, NS), R("idb"), R("mx", 7, 8 * NS, 8), False, True)
+        mm(R(P6, 0, B - NS), R("idb"), R("mx", 8 * NS + 7, 8 * B, 8), False, True)
+        act(R("zo", zo, zo + NS), R(PK, 0, NS), Act.Abs)
+        act(R("zo", zo + NS, zo + B), R(P6, 0, B - NS), Act.Abs)
+        zo = R("zo", zo, zo + B)
+        send(nxt, R("yb", y0 + 336, y0 + 336 + B), zo, "zr%d" % n)
+        if n == 0:
+            lines_of(3)
+            fill(R("wt", W, WT), 0.0)
+            fill(R("q25"), 0.25)
+            fill(R("on32"), 1.0 / 32)
+            cp(R("iob"), R("im", 0, B))
+            tt(R("g8"), R("pg", 0, 8), R("im", 0, 8), Op.is_equal)
+            for j in range(4):
+                waits_of(j)
+            ts(S7("c1"), S7("iw"), BIG, Op.add)
+            ts(S7("cwn"), S7("iw"), -256.0, Op.mult, -256.0 * W, Op.add)
+            ts(R("lbx", 8, 15), S7("iw"), 16.0, Op.mult, BIG, Op.add)
+        else:
+            tt(R("rz"), R("wdm"), z, Op.add)
+            ts(R("ry"), R("rz"), 31, Op.bitwise_and)
+            cp(IND(R("wt"), S7("doff")), R("ry"))
+        if n < 7:
+            mm(R(P7, 0, B), R("nid"), z, True, False)
+            mm(R(P7, 0, B), R("idb"), zo, False, True)
+            act(R("ge2"), R(P7, 0, B), Act.Sign, 0.5)
+            mm(R(P7, B, 2 * B), R("gb"), R("ge2"), True, True)
+            act(R("jk"), R(P7, B, 2 * B), Act.Sign, -1.0, R("acc"))
+            mm(R(P7, 256, 257), R("on32"), R("acc"), True, False)
+            mm(R(P7, 256, 257), R("on32"), R("q25"), False, True)
+            act(R("af1"), R(P7, 256, 257), Act.Identity, MAGIC)
+            act(R("af2"), R("af1"), Act.Identity, MAGIC, scale=-1.0)
+            act(R("av", n + 1, n + 2), R(P7, 256, 257), Act.Identity, R("af2"))
+        mm(R(P7, 264, 272, p=B), zo, R("g8"), True, True)
+        act(R("sall", 8 * n, 8 * n + 8, p=B), R(P7, 264, 272, p=B), Act.Copy)
+        if n >= 6:
+            m0, m1 = (0, 3) if n == 6 else (3, 4)
+            hi = n + 1
+            cp(R("si", 0, 8 * hi, p=B), R("sall", 0, 8 * hi, p=B))
+            ts(R("ai", 0, hi), R("av", 0, hi), -1.0, Op.add)
+            ts(R("sj", 0, 8 * hi, p=B), R("si", 0, 8 * hi, p=B), 31, Op.bitwise_and)
+            ts(R("aj", 0, hi), R("ai", 0, hi), 31, Op.bitwise_and)
+            tt(R("pp", 8 * m0, 8 * m1, p=B), R("sj", 8 * m0, 8 * m1, p=B), R("sj", 8 * m0 + 32, 8 * m1 + 32, p=B), Op.add)
+            tt(R("af", m0, m1), R("aj", m0, m1), R("aj", m0 + 4, m1 + 4), Op.add)
+            if n == 6:
+                fill(R("pt"), 0.0)
+            for j in range(m0, m1):
+                ts(R("pt", 8 * j, 8 * j + 8, p=B), R("pp", 8 * j, 8 * j + 8, p=B), R("af", j, j + 1, p=B), Op.add, 2.0, Op.add)
+                if j > 0:
+                    send(cores[(rank - j) % NR], R("tpa", 8 * j, 8 * j + 8), R("pt", 8 * j, 8 * j + 8), "tp%d" % j)
+
+    tt(R("rz"), R("wdm"), z, Op.add)
+    ts(R("ry"), R("rz"), 31, Op.bitwise_and)
+    cp(IND(R("wt"), S7("doff")), R("ry"))
+    dma("Y", T.yw[:, :], T.wt[:, 0:W], [("wt", 0, W)], [])
+    dma("S", T.yy[:, :], T.yb[:, y0:y0 + B], z[1], [])
+    ts(R("fs"), R(PQ, 0, B), 1.0, Op.is_ge)
+    tt(R("fd"), R("fs"), R(P6, B, 2 * B), Op.mult)
+    tt(R("fl"), R("fd"), R(P6, 0, B), Op.add)
+    ts(R("fy"), R("fl"), 1.0 / 32, Op.mult)
+    dma("S", T.yl[:, :], T.fy[0:128:16, :], [("fy", 0, B)], [])
+    for j in range(1, 4):
+        landed("tp%d" % j, cores[(rank + j) % NR], [("tpa", 8 * j, 8 * j + 8)])
+    idq = (T.idf[0:B, 0:B], [("idf", 0, B)], [])
+    for j in range(4):
+        mm(R(P1, 0, B, p=8), R("pt" if j == 0 else "tpa", 8 * j, 8 * j + 8, p=B), idq, j == 0, j == 3)
+    tt(R("ft", p=8), R("tki", p=8), R(P1, 0, B, p=8), Op.add)
+    ts(R("fu", p=8), R("ft", p=8), 4095, Op.bitwise_and)
+    cp(R("fv", p=8), R("fu", p=8))
+    dma("Y", T.yt[:, :], T.fv[0:8, :], [("fv", 0, B)], [])
+    for q in ("V", "S", "P", "G"):
+        g.wait_ge(T.sem[sems[q]], cnt[q])
+    for name in dma_all:
+        g.wait_ge(T.sem[name], 16)
+    g.wait_ge(T.sem.lsem, sent[0])

@@ -3,7 +3,7 @@ from concourse.mybir import AluOpType as Op, ActivationFunctionType as Act
 NR, B, W, STEPS = 4, 112, 1920, 8
 BIG = float(3 * 2 ** 21)
 MAGIC = float(3 * 2 ** 27)
-NV, N1 = 34, 58
+CH = (0, 20, 48, 80, B)
 WT = W + B
 
 SCRATCH = {}
@@ -11,18 +11,20 @@ for _names, _w, _t in (
         ("xt lt", W, "bfloat16"), ("wt", WT, "bfloat16"), ("ili", W, "int32"), ("lf lg", W, "float32"),
         ("tki lni ci cl ui u5 rz ry ft fu", B, "int32"),
         ("t0f l0f mk1 qw uf fs fd fl fy fv", B, "float32"),
-        ("mkb iob wdm ge ge2 jk ug wf", B, "bfloat16"), ("so", B, "uint16"),
-        ("ip im pg mg p15 m15", 128, "int32"), ("idf onf s15 e8f on32", 128, "float32"),
-        ("idb nid gb gs se0 se1 nse onb", 128, "bfloat16"),
+        ("mkb iob wdm ge ge2 jk ug wf", B, "bfloat16"),
+        ("ip im pg mg p15 m15", 128, "int32"), ("idf e8f on32", 128, "float32"),
+        ("onf s15 idb nid gb gs se0 se1 nse onb", 128, "bfloat16"),
         ("g8", 8, "bfloat16"), ("q16 ai aj", 8, "int32"), ("iw c1 cwn nb lose tp8 mn dl sk sd av", 8, "float32"), ("doff", 8, "uint16"),
         ("acc af1 af2 q25", 1, "float32"), ("af", 4, "float32"),
         ("qi tq", 16, "int32"), ("lbx ta", 16, "float32"), ("offs", 16, "uint16"),
         ("r3 w3", 3 * B, "float32"), ("rd eq em", 7 * B, "bfloat16"),
-        ("rp", 16 * N1, "bfloat16"), ("r8", 8 * N1, "bfloat16"), ("vb pm", 16 * B, "bfloat16"), ("mx", 8 * B, "bfloat16"),
+        ("r8", 8 * 44, "bfloat16"), ("vo mn2 mx", 8 * B, "bfloat16"), ("xr", B, "bfloat16"), ("sev sod", 56, "uint16"), ("nk", 8, "float32"),
+        ("elo ehi olo ohi", 128, "bfloat16"),
         ("sall", 64, "float32"), ("si sj", 64, "int32"), ("pp pt tpa", 32, "float32"),
-        ("yb", 9 * 336, "bfloat16"),
-        ("ey", 8 * 336, "bfloat16"),
-        ("zo", 8 * B, "bfloat16"), ("eo es", 8 * B, "float32")):
+        ("yb", 9 * 224, "bfloat16"),
+        ("lr", 8 * 224, "bfloat16"),
+        ("ey er", 8 * 224, "bfloat16"),
+        ("zo", 8 * B, "bfloat16"), ("eo", B, "float32"), ("flx k15", B, "bfloat16"), ("dof0", 8, "uint16")):
     for _n in _names.split():
         SCRATCH[_n] = ("sbuf", [128, _w], _t)
 PSUM = ["b%d" % i for i in range(8)]
@@ -174,15 +176,14 @@ def rank_program(g, core, T, topo):
         else:
             emit("G", [], out[1], lambda: g.iota(out[0], pat, base, cm))
 
-    def pick(out, ones, base):
-        emit("G", ones[1], out[1], lambda: g.affine_select(out=out[0], in_=ones[0], pattern=[[-16, 8], [0, 16]], compare_op=Op.is_equal,
+    def pick(out, ones, base, st=0):
+        emit("G", ones[1], out[1], lambda: g.affine_select(out=out[0], in_=ones[0], pattern=[[-16, 8], [st, 16]], compare_op=Op.is_equal,
                                                            fill=0.0, base=base, channel_multiplier=1))
     iota(R("ip"), [[0, 128]], 0, 1)
     iota(R("im"), [[1, 128]], 0, 0)
     fill(R("onb"), 1.0)
     fill(R("r3"), float(2 ** 24))
     fill(R("r3", 0, 3 * B, 16), 0.0)
-    iota(R("rp"), [[0, 8 * N1], [-255, 2]], 255, 0, True)
     pick(R("se0"), R("onb"), 0)
     pick(R("se1"), R("onb"), -1)
     fill(R("onf"), 256.0)
@@ -208,11 +209,14 @@ def rank_program(g, core, T, topo):
     mm(R(PW, B, 2 * B), E8, R("l0f", p=8), False, True)
     fill(R("av"), 1.0)
     fill(R("r8"), 255.0)
-    fill(R("r8", 0, 8 * N1, 8), 0.0)
+    fill(R("r8", 0, 8 * 44, 8), 0.0)
+    fill(R("k15"), 15.5)
     fill(R("tq"), 0)
     fill(R("lbx"), BIG)
     ts(R("pg"), R("ip"), 4, Op.arith_shift_right)
     tt(R("gb"), R("pg"), R("mg"), Op.is_equal)
+    for nm, base in (("elo", 0), ("ehi", 16), ("olo", -1), ("ohi", 15)):
+        pick(R(nm), R("gb"), base, -2)
     act(R("gs"), R("gb"), Act.Copy, scale=float(2 ** 17))
     fill(R("rd"), 0.0)
     fill(R("rd", 0, 784, 112), 4096.0)
@@ -231,30 +235,58 @@ def rank_program(g, core, T, topo):
         bank = (PL, PW, PZ, PK)[j]
         mm(R(bank, 0, C4), R("idb"), R("lt", a, b), True, True)
         tt(R("wt", a, b), R("ili", a, b), R(bank, 0, C4), Op.subtract)
-    for j in range(3):
-        lines_of(j)
 
     SEG = lambda name, k=0: R(name, k * B + 15, (k + 1) * B, 16)
     S7 = lambda name: R(name, 0, 7)
-    NS = NV + N1
+
+    def parts_of(n):
+        m0, m1 = (0, 3) if n == 6 else (3, 4)
+        hi = n + 1
+        cp(R("si", 0, 8 * hi, p=B), R("sall", 0, 8 * hi, p=B))
+        ts(R("ai", 0, hi), R("av", 0, hi), -1.0, Op.add)
+        ts(R("sj", 0, 8 * hi, p=B), R("si", 0, 8 * hi, p=B), 31, Op.bitwise_and)
+        ts(R("aj", 0, hi), R("ai", 0, hi), 31, Op.bitwise_and)
+        tt(R("pp", 8 * m0, 8 * m1, p=B), R("sj", 8 * m0, 8 * m1, p=B), R("sj", 8 * m0 + 32, 8 * m1 + 32, p=B), Op.add)
+        tt(R("af", m0, m1), R("aj", m0, m1), R("aj", m0 + 4, m1 + 4), Op.add)
+        if n == 6:
+            fill(R("pt"), 0.0)
+        for j in range(m0, m1):
+            ts(R("pt", 8 * j, 8 * j + 8, p=B), R("pp", 8 * j, 8 * j + 8, p=B), R("af", j, j + 1, p=B), Op.add, 2.0, Op.add)
+            if j > 0:
+                send(cores[(rank - j) % NR], R("tpa", 8 * j, 8 * j + 8), R("pt", 8 * j, 8 * j + 8), "tp%d" % j)
+
+    def tail_of(n):
+        if n < 7:
+            mm(R(P7, 256, 257), R("on32"), R("q25"), True, False)
+            mm(R(P7, 256, 257), R("on32"), R("acc"), False, True)
+            act(R("af1"), R(P7, 256, 257), Act.Identity, MAGIC)
+            act(R("af2"), R("af1"), Act.Identity, MAGIC, scale=-1.0)
+            act(R("av", n + 1, n + 2), R(P7, 256, 257), Act.Identity, R("af2"))
+        mm(R(P7, 264, 272, p=B), R("zo", B * n, B * n + B), R("g8"), True, True)
+        act(R("sall", 8 * n, 8 * n + 8, p=B), R(P7, 264, 272, p=B), Act.Copy)
+        if n >= 6:
+            parts_of(n)
 
     for n in range(STEPS + 1):
         last = n == STEPS
-        y0 = 336 * n
-        z, lns, clk = R("yb", y0, y0 + B), R("yb", y0 + B, y0 + 2 * B), R("yb", y0 + 2 * B, y0 + 3 * B)
+        y0 = 224 * n
+        z, clk = R("yb", y0, y0 + B), R("yb", y0 + B, y0 + 2 * B)
+        lns, rot = (None, None) if last else (R("lr", y0, y0 + B), R("lr", y0 + B, y0 + 2 * B))
         if n > 0:
             k = n - 1
-            e0 = 336 * k
-            ey, el, ec = R("ey", e0, e0 + B), R("ey", e0 + B, e0 + 2 * B), R("ey", e0 + 2 * B, e0 + 3 * B)
-            es = R("es", B * k, B * k + B)
-            landed("ea%d" % k, prv, [("ey", e0, e0 + (336 if k < 7 else 224))])
-            landed("eb%d" % k, prv, es[1])
+            e0 = 224 * k
+            ey, ec = R("ey", e0, e0 + B), R("ey", e0 + B, e0 + 2 * B)
+            el, et = R("er", e0, e0 + B), R("er", e0 + B, e0 + 2 * B)
+            landed("ea%d" % k, prv, [("ey", e0, e0 + (224 if k < 7 else 112))])
+            landed("eb%d" % k, prv, [("er", e0, e0 + 224)])
             KM = R(P6, 256, 256 + B)
             mm(KM, R("idb"), R("mkb"), True, False)
             mm(KM, R("idb"), R("iob"), False, False)
-            mm(KM, R("s15"), es, False, True)
             mm(R(PK, 0, B), R("idb"), R("iob"), True, False)
-            mm(R(PK, 0, B), R("s15"), es, False, True)
+            mm(KM, R("s15"), el, False, False)
+            mm(KM, R("s15"), et, False, True)
+            mm(R(PK, 0, B), R("s15"), el, False, False)
+            mm(R(PK, 0, B), R("s15"), et, False, True)
             for c in (0, B):
                 mm(R(PW, c, c + B), R("idb"), R("mkb"), True, False)
                 if c:
@@ -265,25 +297,31 @@ def rank_program(g, core, T, topo):
                 mm(R(PQ, 0, B), R("idb"), R("mkb"), True, False)
                 mm(R(PQ, 0, B), R("idb"), ec, False, False)
                 mm(R(P1, 0, B), R("idb"), ec, True, False)
+                UC = R(P7, 280, 280 + B)
+                PX, PE, PO, PR = R(PW, 256, 256 + B), R(PL, 0, 56), R(PZ, 128, 184), R(P6, 128, 128 + B)
             scan(R("w3", 0, B), R("r3", 0, B), KM, 0.0, Op.min, Op.max)
             tt(S7("nb"), S7("c1"), SEG("w3"), Op.subtract)
             for q in range(7):
                 L = 16 * q + 16
                 act(R("eq", 112 * q + 112 - L, 112 * q + 112), R(PK, 0, L), Act.Abs, R("nb", q, q + 1))
-            scan(R("w3", B, 3 * B), R("r3", B, 3 * B), R(PW, 0, 2 * B), 0.0, Op.min, Op.max)
+            ts(S7("dof0"), S7("nb"), -1.0 / 256, Op.mult)
+            ts(S7("nk"), S7("nb"), 2.0 ** -20, Op.mult)
+            ts(R("wdm"), IND(R("wt"), S7("dof0")), -32.0, Op.add)
+            tt(S7("nk"), S7("nk"), S7("iw"), Op.subtract)
             scan(R("em", 0, 448), R("rd", 0, 448), R("eq", 0, 448), 4096.0, Op.max, Op.min)
+            scan(R("em", 448, 784), R("rd", 448, 784), R("eq", 448, 784), 4096.0, Op.max, Op.min)
+            scan(R("w3", B, 3 * B), R("r3", B, 3 * B), R(PW, 0, 2 * B), 0.0, Op.min, Op.max)
+            tt(S7("tp8"), R("em", 111, 784, 112), S7("nk"), Op.add)
             ts(S7("dl"), SEG("w3", 2), -BIG, Op.add)
             cp(S7("lbx"), SEG("w3", 1))
-            scan(R("em", 448, 784), R("rd", 448, 784), R("eq", 448, 784), 4096.0, Op.max, Op.min)
-            tt(S7("lose"), R("em", 111, 784, 112), S7("iw"), Op.is_lt)
-            tt(S7("tp8"), S7("lose"), S7("cwn"), Op.mult)
-            tt(S7("mn"), S7("nb"), S7("tp8"), Op.min)
-            ts(S7("doff"), S7("mn"), -1.0 / 256, Op.mult)
-            ts(R("wdm"), IND(R("wt"), S7("doff")), -32.0, Op.add)
+            tt(S7("mn"), S7("tp8"), S7("cwn"), Op.max)
+            ts(S7("doff"), S7("mn"), -4096.0, Op.mult)
             if last:
                 mm(R(P6, 0, B), R("se0"), el, True, True)
                 mm(R(P6, B, 2 * B), R("se1"), el, True, False)
                 mm(R(P6, B, 2 * B), R("nse"), el, False, True)
+            if not last:
+                tail_of(k)
             landed("zr%d" % k, prv, z[1])
             mm(R(PZ, 0, B), R("idb"), z, False, True)
             if not last:
@@ -292,6 +330,10 @@ def rank_program(g, core, T, topo):
                 tt(IND(R("wt"), S7("doff")), R("wdm"), z, Op.add)
             act(R("ge"), R(PZ, 0, B), Act.Sign, 0.5)
             mm(R(PQ, 0, B), R("gb" if last else "gs"), R("ge"), last, True)
+            if not last:
+                mm(UC, R("idb"), ec, True, False)
+                mm(UC, R("gb"), z, False, False)
+                mm(PX, R("idb"), R("k15"), True, False)
         if last:
             break
         scan(R("qw"), R("r3", 0, B), R(PQ, 0, B), 0.0, Op.min, Op.max)
@@ -310,55 +352,86 @@ def rank_program(g, core, T, topo):
         if n > 0:
             tt(S7("ta"), S7("ta"), S7("sd"), Op.add)
         ts(R("offs", 0, E), R("ta", 0, E), -BIG, Op.add)
-        if n < 7:
-            act(R("uf"), R(P1, 0, B), Act.Identity, MAGIC)
-            act(R("ug"), R("uf"), Act.Identity, -MAGIC)
+        act(R("uf"), R(P1, 0, B), Act.Identity, MAGIC)
+        act(R("ug"), R("uf"), Act.Identity, -MAGIC)
+        if n == 0:
             UC = R(P7, 280, 280 + B)
-            if n > 0:
-                mm(UC, R("idb"), ec, True, False)
-                mm(UC, R("gb"), z, False, False)
-            else:
-                mm(UC, E8, R("t0f", p=8), True, False)
-            mm(UC, R("nid"), R("ug"), False, True)
+            mm(UC, E8, R("t0f", p=8), True, False)
+        mm(UC, R("nid"), R("ug"), False, True)
+        if n > 0:
+            act(R("xr"), UC, Act.Copy)
+        if n < 7:
             act(clk, UC, Act.Identity, R("av", n, n + 1))
-        so = R("eo", B * n, B * n + B)
         if n > 0:
             act(R("wf"), IND(R("wt"), S7("offs")), Act.Copy)
             act(lns, IND(R("lt"), S7("offs")), Act.Copy)
             cp(IND(R("xt"), R("offs", 8, 15)), z)
-            mm(R(PL, 0, B), R("idb"), lns, True, True)
-            tt(R("ui"), R("wf"), R(P1, 0, B), Op.add)
-            ts(R("u5"), R("ui"), 31, Op.bitwise_and)
-            tt(so, R("u5"), R(PL, 0, B), Op.add)
+            lists = ((PO, "olo", "ohi"), (PE, "elo", "ehi"))
+
+            def halves(pb, lo, hi, name, a, start, stop):
+                mm(pb, R(lo), R(name, a, a + B, 2), start, False)
+                mm(pb, R(hi), R(name, a + 1, a + B, 2), False, stop)
+            for pb, lo, hi in lists:
+                halves(pb, lo, hi, "xr", 0, True, False)
+            mm(PR, R("idb"), R("xr"), True, False)
+            mm(PX, R("nid"), R("xr"), False, False)
+            mm(PX, R("nid"), R("wf"), False, True)
+            ts(R("flx"), PX, MAGIC, Op.add, -MAGIC, Op.add)
+            for pb, lo, hi in lists:
+                halves(pb, lo, hi, "wf", 0, False, False)
+            mm(PR, R("idb"), R("wf"), False, False)
+            halves(PO, "olo", "ohi", "lr", y0, False, False)
+            halves(PO, "olo", "ohi", "flx", 0, False, True)
+            mm(PR, R("idb"), R("flx"), False, True)
+            halves(PE, "elo", "ehi", "lr", y0, False, False)
+            halves(PE, "elo", "ehi", "flx", 0, False, True)
+            cp(R("sod"), PO)
+            cp(R("sev"), PE)
+            act(rot, PR, Act.Copy)
         else:
+            for j in range(2):
+                lines_of(j)
             cp(R("ci"), IND(R("ili"), S7("offs")))
             tt(R("ui"), R("ci"), R(P1, 0, B), Op.add)
             ts(R("cl"), R("ci"), 4064, Op.bitwise_and)
             ts(R("u5"), R("ui"), 31, Op.bitwise_and)
-            tt(so, R("u5"), R("cl"), Op.add)
-        cp(R("so"), so)
-        if n == 0:
             cp(lns, R("cl"))
-        send(nxt, R("es", B * n, B * n + B), so, "eb%d" % n)
-        ew = 336 if n < 7 else 224
-        send(nxt, R("ey", y0, y0 + ew), R("yb", y0, y0 + ew), "ea%d" % n)
-        act(R("vb", 16 * NV, 16 * NS), IND(R("xt"), R("so", NV, NS)), Act.Copy)
-        act(R("vb", 16 * NS, 16 * B), IND(R("xt"), R("so", NS, B)), Act.Copy)
-        cp(R("vb", 0, 16 * NV), IND(R("xt"), R("so", 0, NV)))
-        mm(R(PK, 0, NS), R("nid"), R("yb", y0, y0 + NS), True, False)
-        mm(R(P6, 0, B - NS), R("nid"), R("yb", y0 + NS, y0 + B), True, False)
-        for a, b in ((0, NV), (NV, NS), (NS, B)):
-            w = b - a
-            scan(R("pm", 16 * a, 16 * b), R("rp", 0, 16 * w), R("vb", 16 * a, 16 * b), 255.0, Op.max, Op.min)
-            scan(R("mx", 8 * a, 8 * b), R("r8", 0, 8 * w), R("pm", 16 * a + 1, 16 * b, 2), 0.0, Op.min, Op.max)
+            cp(rot, R("u5"))
+            for pb, lo, hi, od in ((R(PZ, 128, 184), "olo", "ohi", "sod"), (R(PL, 0, 56), "elo", "ehi", "sev")):
+                for o in (0, B):
+                    mm(pb, R(lo), R("lr", o, o + B, 2), o == 0, False)
+                    mm(pb, R(hi), R("lr", o + 1, o + B, 2), False, o > 0)
+                cp(R(od), pb)
+        for a, b in zip(CH, CH[1:]):
+            act(R("vo", 8 * a, 8 * b), IND(R("xt"), R("sod", a // 2, b // 2)), Act.Copy)
+            if a == 0:
+                send(nxt, R("er", y0, y0 + 224), R("lr", y0, y0 + 224), "eb%d" % n)
+                ew = 224 if n < 7 else 112
+                send(nxt, R("ey", y0, y0 + ew), R("yb", y0, y0 + ew), "ea%d" % n)
+        M = CH[-3]
+        mm(R(PK, 0, M), R("nid"), R("yb", y0, y0 + M), True, False)
+        mm(R(P6, 0, B - M), R("nid"), R("yb", y0 + M, y0 + B), True, False)
+
+        def least(k):
+            a, b = CH[k], CH[k + 1]
+            tt(R("mn2", 8 * a, 8 * b), IND(R("xt"), R("sev", a // 2, b // 2)), R("vo", 8 * a, 8 * b), Op.min)
+
+        def greatest(a, b):
+            scan(R("mx", 8 * a, 8 * b), R("r8", 0, 8 * (b - a)), R("mn2", 8 * a, 8 * b), 0.0, Op.min, Op.max)
+        for k in range(len(CH) - 1):
+            least(k)
+            if k > 0:
+                greatest(CH[k - 1], CH[k])
+        greatest(CH[-2], B)
         zo = B * n
-        mm(R(PK, 0, NS), R("idb"), R("mx", 7, 8 * NS, 8), False, True)
-        mm(R(P6, 0, B - NS), R("idb"), R("mx", 8 * NS + 7, 8 * B, 8), False, True)
-        act(R("zo", zo, zo + NS), R(PK, 0, NS), Act.Abs)
-        act(R("zo", zo + NS, zo + B), R(P6, 0, B - NS), Act.Abs)
+        mm(R(PK, 0, M), R("idb"), R("mx", 7, 8 * M, 8), False, True)
+        mm(R(P6, 0, B - M), R("idb"), R("mx", 8 * M + 7, 8 * B, 8), False, True)
+        act(R("zo", zo, zo + M), R(PK, 0, M), Act.Abs)
+        act(R("zo", zo + M, zo + B), R(P6, 0, B - M), Act.Abs)
         zo = R("zo", zo, zo + B)
-        send(nxt, R("yb", y0 + 336, y0 + 336 + B), zo, "zr%d" % n)
+        send(nxt, R("yb", y0 + 224, y0 + 224 + B), zo, "zr%d" % n)
         if n == 0:
+            lines_of(2)
             lines_of(3)
             fill(R("wt", W, WT), 0.0)
             fill(R("q25"), 0.25)
@@ -368,7 +441,7 @@ def rank_program(g, core, T, topo):
             for j in range(4):
                 waits_of(j)
             ts(S7("c1"), S7("iw"), BIG, Op.add)
-            ts(S7("cwn"), S7("iw"), -256.0, Op.mult, -256.0 * W, Op.add)
+            ts(S7("cwn"), S7("iw"), -1.0 / 4096, Op.mult, -W / 4096.0, Op.add)
             ts(R("lbx", 8, 15), S7("iw"), 16.0, Op.mult, BIG, Op.add)
         else:
             tt(R("rz"), R("wdm"), z, Op.add)
@@ -380,28 +453,8 @@ def rank_program(g, core, T, topo):
             act(R("ge2"), R(P7, 0, B), Act.Sign, 0.5)
             mm(R(P7, B, 2 * B), R("gb"), R("ge2"), True, True)
             act(R("jk"), R(P7, B, 2 * B), Act.Sign, -1.0, R("acc"))
-            mm(R(P7, 256, 257), R("on32"), R("acc"), True, False)
-            mm(R(P7, 256, 257), R("on32"), R("q25"), False, True)
-            act(R("af1"), R(P7, 256, 257), Act.Identity, MAGIC)
-            act(R("af2"), R("af1"), Act.Identity, MAGIC, scale=-1.0)
-            act(R("av", n + 1, n + 2), R(P7, 256, 257), Act.Identity, R("af2"))
-        mm(R(P7, 264, 272, p=B), zo, R("g8"), True, True)
-        act(R("sall", 8 * n, 8 * n + 8, p=B), R(P7, 264, 272, p=B), Act.Copy)
-        if n >= 6:
-            m0, m1 = (0, 3) if n == 6 else (3, 4)
-            hi = n + 1
-            cp(R("si", 0, 8 * hi, p=B), R("sall", 0, 8 * hi, p=B))
-            ts(R("ai", 0, hi), R("av", 0, hi), -1.0, Op.add)
-            ts(R("sj", 0, 8 * hi, p=B), R("si", 0, 8 * hi, p=B), 31, Op.bitwise_and)
-            ts(R("aj", 0, hi), R("ai", 0, hi), 31, Op.bitwise_and)
-            tt(R("pp", 8 * m0, 8 * m1, p=B), R("sj", 8 * m0, 8 * m1, p=B), R("sj", 8 * m0 + 32, 8 * m1 + 32, p=B), Op.add)
-            tt(R("af", m0, m1), R("aj", m0, m1), R("aj", m0 + 4, m1 + 4), Op.add)
-            if n == 6:
-                fill(R("pt"), 0.0)
-            for j in range(m0, m1):
-                ts(R("pt", 8 * j, 8 * j + 8, p=B), R("pp", 8 * j, 8 * j + 8, p=B), R("af", j, j + 1, p=B), Op.add, 2.0, Op.add)
-                if j > 0:
-                    send(cores[(rank - j) % NR], R("tpa", 8 * j, 8 * j + 8), R("pt", 8 * j, 8 * j + 8), "tp%d" % j)
+        else:
+            tail_of(n)
 
     tt(R("rz"), R("wdm"), z, Op.add)
     ts(R("ry"), R("rz"), 31, Op.bitwise_and)

@@ -203,21 +203,20 @@ def rank_program(g, core, T, topo):
     P1, PQ, PZ, PL, PK, PW, P6, P7 = PSUM
     E8 = R("e8f", p=8)
     mm(R(P1, 0, B), E8, R("t0f", p=8), True, True)
+    fill(R("k15"), 15.5)
     mm(R(PQ, 0, B), R("idb"), R("mkb"), True, False)
+    mm(R(PQ, 0, B), R("nid"), R("k15"), False, False)
     mm(R(PQ, 0, B), E8, R("t0f", p=8), False, True)
     mm(R(PW, B, 2 * B), R("idb"), R("mkb"), True, False)
     mm(R(PW, B, 2 * B), E8, R("l0f", p=8), False, True)
     fill(R("av"), 1.0)
     fill(R("r8"), 255.0)
     fill(R("r8", 0, 8 * 44, 8), 0.0)
-    fill(R("k15"), 15.5)
-    fill(R("tq"), 0)
-    fill(R("lbx"), BIG)
     ts(R("pg"), R("ip"), 4, Op.arith_shift_right)
     tt(R("gb"), R("pg"), R("mg"), Op.is_equal)
     for nm, base in (("elo", 0), ("ehi", 16), ("olo", -1), ("ohi", 15)):
         pick(R(nm), R("gb"), base, -2)
-    act(R("gs"), R("gb"), Act.Copy, scale=float(2 ** 17))
+    act(R("gs"), R("gb"), Act.Copy, scale=float(2 ** 16))
     fill(R("rd"), 0.0)
     fill(R("rd", 0, 784, 112), 4096.0)
     fill(R("eq"), 4096.0)
@@ -227,12 +226,15 @@ def rank_program(g, core, T, topo):
     def lines_of(j):
         a, b = j * C4, (j + 1) * C4
         ts(R("lf", a, b), R("ili", a, b), -15.5, Op.add)
+
+    def lines_act(j):
+        a, b = j * C4, (j + 1) * C4
         act(R("lg", a, b), R("lf", a, b), Act.Identity, MAGIC)
         act(R("lt", a, b), R("lg", a, b), Act.Identity, -MAGIC)
 
     def waits_of(j):
         a, b = j * C4, (j + 1) * C4
-        bank = (PL, PW, PZ, PK)[j]
+        bank = (PW, PL, PZ, PQ)[j]
         mm(R(bank, 0, C4), R("idb"), R("lt", a, b), True, True)
         tt(R("wt", a, b), R("ili", a, b), R(bank, 0, C4), Op.subtract)
 
@@ -257,13 +259,9 @@ def rank_program(g, core, T, topo):
 
     def tail_of(n):
         if n < 7:
-            mm(R(P7, 256, 257), R("on32"), R("q25"), True, False)
-            mm(R(P7, 256, 257), R("on32"), R("acc"), False, True)
             act(R("af1"), R(P7, 256, 257), Act.Identity, MAGIC)
             act(R("af2"), R("af1"), Act.Identity, MAGIC, scale=-1.0)
             act(R("av", n + 1, n + 2), R(P7, 256, 257), Act.Identity, R("af2"))
-        mm(R(P7, 264, 272, p=B), R("zo", B * n, B * n + B), R("g8"), True, True)
-        act(R("sall", 8 * n, 8 * n + 8, p=B), R(P7, 264, 272, p=B), Act.Copy)
         if n >= 6:
             parts_of(n)
 
@@ -280,13 +278,12 @@ def rank_program(g, core, T, topo):
             landed("ea%d" % k, prv, [("ey", e0, e0 + (224 if k < 7 else 112))])
             landed("eb%d" % k, prv, [("er", e0, e0 + 224)])
             KM = R(P6, 256, 256 + B)
-            mm(KM, R("idb"), R("mkb"), True, False)
-            mm(KM, R("idb"), R("iob"), False, False)
-            mm(R(PK, 0, B), R("idb"), R("iob"), True, False)
             mm(KM, R("s15"), el, False, False)
             mm(KM, R("s15"), et, False, True)
             mm(R(PK, 0, B), R("s15"), el, False, False)
             mm(R(PK, 0, B), R("s15"), et, False, True)
+            if not last:
+                mm(R(P7, B, 2 * B), R("gb"), R("ge2"), True, True)
             for c in (0, B):
                 mm(R(PW, c, c + B), R("idb"), R("mkb"), True, False)
                 if c:
@@ -295,6 +292,7 @@ def rank_program(g, core, T, topo):
             mm(R(PZ, 0, B), R("nid"), ey, True, False)
             if not last:
                 mm(R(PQ, 0, B), R("idb"), R("mkb"), True, False)
+                mm(R(PQ, 0, B), R("nid"), R("k15"), False, False)
                 mm(R(PQ, 0, B), R("idb"), ec, False, False)
                 mm(R(P1, 0, B), R("idb"), ec, True, False)
                 UC = R(P7, 280, 280 + B)
@@ -313,7 +311,7 @@ def rank_program(g, core, T, topo):
             scan(R("w3", B, 3 * B), R("r3", B, 3 * B), R(PW, 0, 2 * B), 0.0, Op.min, Op.max)
             tt(S7("tp8"), R("em", 111, 784, 112), S7("nk"), Op.add)
             ts(S7("dl"), SEG("w3", 2), -BIG, Op.add)
-            cp(S7("lbx"), SEG("w3", 1))
+            ts(S7("lbx"), SEG("w3", 1), -BIG, Op.add)
             tt(S7("mn"), S7("tp8"), S7("cwn"), Op.max)
             ts(S7("doff"), S7("mn"), -4096.0, Op.mult)
             if last:
@@ -321,7 +319,11 @@ def rank_program(g, core, T, topo):
                 mm(R(P6, B, 2 * B), R("se1"), el, True, False)
                 mm(R(P6, B, 2 * B), R("nse"), el, False, True)
             if not last:
-                tail_of(k)
+                act(R("jk"), R(P7, B, 2 * B), Act.Sign, -1.0, R("acc"))
+                mm(R(P7, 256, 257), R("on32"), R("q25"), True, False)
+                mm(R(P7, 256, 257), R("on32"), R("acc"), False, True)
+                if n == 7:
+                    tail_of(k)
             landed("zr%d" % k, prv, z[1])
             mm(R(PZ, 0, B), R("idb"), z, False, True)
             if not last:
@@ -339,19 +341,22 @@ def rank_program(g, core, T, topo):
         scan(R("qw"), R("r3", 0, B), R(PQ, 0, B), 0.0, Op.min, Op.max)
         if n == 0:
             scan(R("w3", B, 2 * B), R("r3", B, 2 * B), R(PW, B, 2 * B), 0.0, Op.min, Op.max)
-            cp(S7("lbx"), SEG("w3", 1))
-        cp(S7("qi"), SEG("qw"))
+            ts(S7("lbx"), SEG("w3", 1), -BIG, Op.add)
+        tt(S7("ta"), SEG("qw"), S7("lbx"), Op.add)
         if n > 0:
-            ts(S7("sk"), SEG("qw"), BIG + 2.0 ** 17, Op.is_ge)
-        ts(S7("tq"), S7("qi"), 31, Op.bitwise_and)
+            ts(S7("sk"), SEG("qw"), BIG + 2.0 ** 16, Op.is_ge)
+        ts(S7("mn"), SEG("qw"), MAGIC, Op.add, -MAGIC, Op.add)
         if n > 0:
-            ts(R("tq", 8, 15), S7("qi"), 15, Op.bitwise_and)
+            ts(S7("qi"), SEG("qw"), 15.5, Op.add)
             tt(S7("sd"), S7("sk"), S7("dl"), Op.mult)
-        E = 15 if n > 0 else 7
-        tt(R("ta", 0, E), R("tq", 0, E), R("lbx", 0, E), Op.add)
+        tt(S7("ta"), S7("ta"), S7("mn"), Op.subtract)
         if n > 0:
+            ts(S7("tq"), S7("qi"), 15, Op.bitwise_and)
             tt(S7("ta"), S7("ta"), S7("sd"), Op.add)
-        ts(R("offs", 0, E), R("ta", 0, E), -BIG, Op.add)
+            tt(R("ta", 8, 15), S7("tq"), R("lbx", 8, 15), Op.add)
+        ts(S7("offs"), S7("ta"), 15.5, Op.add)
+        if n > 0:
+            cp(R("offs", 8, 15), R("ta", 8, 15))
         act(R("uf"), R(P1, 0, B), Act.Identity, MAGIC)
         act(R("ug"), R("uf"), Act.Identity, -MAGIC)
         if n == 0:
@@ -360,11 +365,14 @@ def rank_program(g, core, T, topo):
         mm(UC, R("nid"), R("ug"), False, True)
         if n > 0:
             act(R("xr"), UC, Act.Copy)
-        if n < 7:
-            act(clk, UC, Act.Identity, R("av", n, n + 1))
         if n > 0:
             act(R("wf"), IND(R("wt"), S7("offs")), Act.Copy)
             act(lns, IND(R("lt"), S7("offs")), Act.Copy)
+            if n < 7:
+                tail_of(n - 1)
+        if n < 7:
+            act(clk, UC, Act.Identity, R("av", n, n + 1))
+        if n > 0:
             cp(IND(R("xt"), R("offs", 8, 15)), z)
             lists = ((PO, "olo", "ohi"), (PE, "elo", "ehi"))
 
@@ -377,20 +385,30 @@ def rank_program(g, core, T, topo):
             mm(PX, R("nid"), R("xr"), False, False)
             mm(PX, R("nid"), R("wf"), False, True)
             ts(R("flx"), PX, MAGIC, Op.add, -MAGIC, Op.add)
-            for pb, lo, hi in lists:
-                halves(pb, lo, hi, "wf", 0, False, False)
-            mm(PR, R("idb"), R("wf"), False, False)
+            halves(PO, "olo", "ohi", "wf", 0, False, False)
             halves(PO, "olo", "ohi", "lr", y0, False, False)
             halves(PO, "olo", "ohi", "flx", 0, False, True)
+            mm(PR, R("idb"), R("wf"), False, False)
             mm(PR, R("idb"), R("flx"), False, True)
+            halves(PE, "elo", "ehi", "wf", 0, False, False)
             halves(PE, "elo", "ehi", "lr", y0, False, False)
             halves(PE, "elo", "ehi", "flx", 0, False, True)
+            tt(R("rz"), R("wdm"), z, Op.add)
             cp(R("sod"), PO)
+            ts(R("ry"), R("rz"), 31, Op.bitwise_and)
             cp(R("sev"), PE)
-            act(rot, PR, Act.Copy)
         else:
-            for j in range(2):
+            fill(R("wt", W, WT), 0.0)
+            fill(R("q25"), 0.25)
+            fill(R("on32"), 1.0 / 32)
+            cp(R("iob"), R("im", 0, B))
+            tt(R("g8"), R("pg", 0, 8), R("im", 0, 8), Op.is_equal)
+            ts(S7("c1"), S7("iw"), BIG, Op.add)
+            ts(S7("cwn"), S7("iw"), -1.0 / 4096, Op.mult, -W / 4096.0, Op.add)
+            ts(R("lbx", 8, 15), S7("iw"), 16.0, Op.mult)
+            for j in range(3):
                 lines_of(j)
+                lines_act(j)
             cp(R("ci"), IND(R("ili"), S7("offs")))
             tt(R("ui"), R("ci"), R(P1, 0, B), Op.add)
             ts(R("cl"), R("ci"), 4064, Op.bitwise_and)
@@ -402,6 +420,10 @@ def rank_program(g, core, T, topo):
                     mm(pb, R(lo), R("lr", o, o + B, 2), o == 0, False)
                     mm(pb, R(hi), R("lr", o + 1, o + B, 2), False, o > 0)
                 cp(R(od), pb)
+            lines_of(3)
+            waits_of(0)
+        if n > 0:
+            act(rot, PR, Act.Copy)
         for a, b in zip(CH, CH[1:]):
             act(R("vo", 8 * a, 8 * b), IND(R("xt"), R("sod", a // 2, b // 2)), Act.Copy)
             if a == 0:
@@ -430,30 +452,23 @@ def rank_program(g, core, T, topo):
         act(R("zo", zo + M, zo + B), R(P6, 0, B - M), Act.Abs)
         zo = R("zo", zo, zo + B)
         send(nxt, R("yb", y0 + 224, y0 + 224 + B), zo, "zr%d" % n)
-        if n == 0:
-            lines_of(2)
-            lines_of(3)
-            fill(R("wt", W, WT), 0.0)
-            fill(R("q25"), 0.25)
-            fill(R("on32"), 1.0 / 32)
-            cp(R("iob"), R("im", 0, B))
-            tt(R("g8"), R("pg", 0, 8), R("im", 0, 8), Op.is_equal)
-            for j in range(4):
-                waits_of(j)
-            ts(S7("c1"), S7("iw"), BIG, Op.add)
-            ts(S7("cwn"), S7("iw"), -1.0 / 4096, Op.mult, -W / 4096.0, Op.add)
-            ts(R("lbx", 8, 15), S7("iw"), 16.0, Op.mult, BIG, Op.add)
-        else:
-            tt(R("rz"), R("wdm"), z, Op.add)
-            ts(R("ry"), R("rz"), 31, Op.bitwise_and)
+        if n > 0:
             cp(IND(R("wt"), S7("doff")), R("ry"))
+        KM = R(P6, 256, 256 + B)
+        mm(KM, R("idb"), R("mkb"), True, False)
+        mm(KM, R("idb"), R("iob"), False, False)
+        mm(R(PK, 0, B), R("idb"), R("iob"), True, False)
+        if n == 0:
+            lines_act(3)
+            for j in range(1, 4):
+                waits_of(j)
         if n < 7:
             mm(R(P7, 0, B), R("nid"), z, True, False)
             mm(R(P7, 0, B), R("idb"), zo, False, True)
             act(R("ge2"), R(P7, 0, B), Act.Sign, 0.5)
-            mm(R(P7, B, 2 * B), R("gb"), R("ge2"), True, True)
-            act(R("jk"), R(P7, B, 2 * B), Act.Sign, -1.0, R("acc"))
-        else:
+        mm(R(PL, 264, 272, p=B), zo, R("g8"), True, True)
+        act(R("sall", 8 * n, 8 * n + 8, p=B), R(PL, 264, 272, p=B), Act.Copy)
+        if n == 7:
             tail_of(n)
 
     tt(R("rz"), R("wdm"), z, Op.add)

from concourse.mybir import AluOpType as Op, ActivationFunctionType as Act

NR, B, W, STEPS = 4, 112, 1920, 8
BIG = float(3 * 2 ** 21)
MAGIC = float(3 * 2 ** 27)
CH = (0, 20, 48, 80, B)
WT = W + B

SCRATCH = {}
for _names, _w, _t in (
        ("xt lt", W, "bfloat16"), ("wt", WT, "bfloat16"), ("ili", W, "int32"), ("lf lg", W, "float32"),
        ("tki lni ci cl ui u5 rz ry ft fu", B, "int32"),
        ("t0f l0f mk1 qw uf fs fd fl fy fv", B, "float32"),
        ("mkb iob wdm ge ge2 jk ug wf", B, "bfloat16"),
        ("ip im pg mg p15 m15", 128, "int32"), ("idf e8f on32", 128, "float32"),
        ("onf s15 idb nid gb gs se0 se1 nse onb", 128, "bfloat16"),
        ("g8", 8, "bfloat16"), ("q16 ai aj", 8, "int32"), ("iw c1 cwn nb lose tp8 mn dl sk sd av", 8, "float32"), ("doff", 8, "uint16"),
        ("acc af1 af2 q25", 1, "float32"), ("af", 4, "float32"),
        ("qi tq", 16, "int32"), ("lbx ta", 16, "float32"), ("offs", 16, "uint16"),
        ("r3 w3", 3 * B, "float32"), ("rd eq em", 7 * B, "bfloat16"),
        ("r8", 8 * 44, "bfloat16"), ("vo mn2 mx", 8 * B, "bfloat16"), ("xr", B, "bfloat16"), ("sev sod", 56, "uint16"), ("nk", 8, "float32"),
        ("elo ehi olo ohi", 128, "bfloat16"),
        ("sall", 64, "float32"), ("si sj", 64, "int32"), ("pp pt tpa", 32, "float32"),
        ("yb", 9 * 224, "bfloat16"),
        ("lr", 8 * 224, "bfloat16"),
        ("ey er", 8 * 224, "bfloat16"),
        ("zo", 8 * B, "bfloat16"), ("eo", B, "float32"), ("flx k15", B, "bfloat16"), ("dof0", 8, "uint16")):
    for _n in _names.split():
        SCRATCH[_n] = ("sbuf", [128, _w], _t)
PSUM = ["b%d" % i for i in range(8)]
for _n in PSUM:
    SCRATCH[_n] = ("psum", [128, 512], "float32")
SEMAPHORES = ["sV", "sS", "sP", "sG", "lsem", "tp1", "tp2", "tp3"] + ["%s%d" % (a, i) for a in ("zr", "ea", "eb") for i in range(8)] + ["d%d" % i for i in range(16)]


def rank_program(g, core, T, topo):
    rank = T.rank_of(core)
    if rank is None:
        return
    cores = T.cores
    nxt, prv = cores[(rank + 1) % NR], cores[(rank - 1) % NR]
    V, S, P = g.vector, g.scalar, g.tensor
    queues = {"V": V, "S": S, "P": P, "G": g, "Y": g.sync}
    sems = {"V": "sV", "S": "sS", "P": "sP", "G": "sG"}
    cnt = {"V": 0, "S": 0, "P": 0, "G": 0}
    know = {q: {} for q in queues}
    clocks = {}
    log = {}

    def ensure(q, need):
        need = {x: i for x, i in need.items() if know[q].get(x, 0) < i}
        for x in list(need):
            if any(y != x and clocks.get((y, j), {}).get(x, 0) >= need[x] for y, j in need.items()):
                del need[x]
        for x, i in need.items():
            queues[q].wait_ge(T.sem[sems.get(x, x)], i)
            for y, j in clocks.get((x, i), {}).items():
                know[q][y] = max(know[q].get(y, 0), j)
            know[q][x] = max(know[q].get(x, 0), i)

    def deps(q, reads, writes):
        need = {}
        for regs, wr in ((reads, False), (writes, True)):
            for name, a, b in regs:
                ps = name in PSUM
                for (c, d, x, i, w) in log.get(name, []):
                    if x == q:
                        if not (w and q != "P" and c < b and a < d):
                            continue
                    elif not (ps or (c < b and a < d and (w or wr))):
                        continue
                    need[x] = max(need.get(x, 0), i)
        return need

    def note(x, i, reads, writes):
        for name, a, b in writes:
            log[name] = [e for e in log.get(name, []) if not (a <= e[0] and e[1] <= b)] + [(a, b, x, i, True)]
        for name, a, b in reads:
            log[name] = [e for e in log.get(name, []) if e[4] or e[2] != x or not (a <= e[0] and e[1] <= b)] + [(a, b, x, i, False)]

    def emit(q, reads, writes, fn):
        ensure(q, deps(q, reads, writes))
        fn().then_inc(T.sem[sems[q]], 1)
        cnt[q] += 1
        c = dict(know[q])
        c[q] = cnt[q]
        clocks[(q, cnt[q])] = c
        note(q, cnt[q], reads, writes)

    def R(name, a=0, b=None, st=1, p=None):
        if b is None:
            b = SCRATCH[name][1][1]
        t = T[name]
        if p is None:
            ap = t[:, a:b] if st == 1 else t[:, a:b:st]
        else:
            ap = t[0:p, a:b] if st == 1 else t[0:p, a:b:st]
        return (ap, [(name, a, b)], [])

    def IND(win, off):
        return (win[0].indirect(off[0]), win[1], off[1])

    def rd(*ops):
        return [r for o in ops if isinstance(o, tuple) for r in o[1] + o[2]]

    def ap(o):
        return o[0] if isinstance(o, tuple) else o

    def tt(out, a, b, op):
        emit("V", rd(a, b) + out[2], out[1], lambda: V.tensor_tensor(out=out[0], in0=a[0], in1=b[0], op=op))

    def ts(out, a, s1, op0, s2=None, op1=None):
        if op1 is None:
            emit("V", rd(a, s1) + out[2], out[1], lambda: V.tensor_scalar(out=out[0], in0=a[0], scalar1=ap(s1), scalar2=None, op0=op0))
        else:
            emit("V", rd(a, s1, s2) + out[2], out[1], lambda: V.tensor_scalar(out=out[0], in0=a[0], scalar1=ap(s1), scalar2=ap(s2), op0=op0, op1=op1))

    def cp(out, a):
        emit("V", rd(a) + out[2], out[1], lambda: V.tensor_copy(out=out[0], in_=a[0]))

    def scan(out, d0, d1, init, op0, op1):
        emit("V", rd(d0, d1), out[1], lambda: V.tensor_tensor_scan(out=out[0], data0=d0[0], data1=d1[0], initial=init, op0=op0, op1=op1))

    def fill(out, v):
        emit("V", [], out[1], lambda: V.memset(out[0], v))

    def act(out, a, f, bias=None, acc=None, scale=None):
        kw = {}
        if scale is not None:
            kw["scale"] = scale
        if bias is not None:
            kw["bias"] = ap(bias)
        if acc is not None:
            kw["accum_out"] = acc[0]
        emit("S", rd(a, bias), out[1] + (acc[1] if acc is not None else []),
             lambda: S.activation(out=out[0], in_=a[0], func=f, **kw))

    def mm(out, l, r, start, stop):
        emit("P", rd(l, r), out[1], lambda: P.matmul(out[0], l[0], r[0], start, stop))

    dma_all = []

    def dma(q, out, src, reads, writes):
        name = "d%d" % len(dma_all)
        ensure(q, deps(q, reads, writes))
        queues[q].dma_start(out=out, in_=src).then_inc(T.sem[name], 16)
        c = dict(know[q])
        c[name] = 16
        clocks[(name, 16)] = c
        note(name, 16, reads, writes)
        dma_all.append(name)

    sent = [0]

    def send(dst, out, src, sem):
        ensure("G", deps("G", src[1], []))
        rid, pid = topo.addr(dst, core)
        m = topo.mask(core, dst)
        g.remote_dma(out_ap=out[0], in_ap=src[0], remote_sem=T.sem[sem], local_sem=T.sem.lsem, pid=pid, routing_id=rid, dma_engine_mask=m)
        sent[0] += len(topo.engines(core, dst))

    def landed(sem, src, regs):
        note(sem, len(topo.engines(src, core)), [], regs)

    dma("Y", T.tki[0:8, :], T.tk0[:, :], [], [("tki", 0, B)])
    dma("S", T.lni[0:8, :], T.ln0[:, :], [], [("lni", 0, B)])
    C4 = W // 4
    for j in range(4):
        dma("YS"[j % 2], T.ili[:, j * C4:(j + 1) * C4], T.il[:, j * C4:(j + 1) * C4], [], [("ili", j * C4, (j + 1) * C4)])
    dma("S", T.xt[:, :], T.xw[:, :], [], [("xt", 0, W)])
    dma("Y", T.yb[:, 0:B], T.y0[:, :], [], [("yb", 0, B)])

    def iota(out, pat, base, cm, flag=False):
        if flag:
            emit("G", [], out[1], lambda: g.iota(out[0], pat, base, cm, allow_small_or_imprecise_dtypes=True))
        else:
            emit("G", [], out[1], lambda: g.iota(out[0], pat, base, cm))

    def pick(out, ones, base, st=0):
        emit("G", ones[1], out[1], lambda: g.affine_select(out=out[0], in_=ones[0], pattern=[[-16, 8], [st, 16]], compare_op=Op.is_equal,
                                                           fill=0.0, base=base, channel_multiplier=1))
    iota(R("ip"), [[0, 128]], 0, 1)
    iota(R("im"), [[1, 128]], 0, 0)
    fill(R("onb"), 1.0)
    fill(R("r3"), float(2 ** 24))
    fill(R("r3", 0, 3 * B, 16), 0.0)
    pick(R("se0"), R("onb"), 0)
    pick(R("se1"), R("onb"), -1)
    fill(R("onf"), 256.0)
    pick(R("s15"), R("onf"), -15)
    tt(R("idb"), R("ip"), R("im"), Op.is_equal)
    ts(R("mg"), R("im"), 4, Op.arith_shift_right)
    ts(R("p15"), R("ip"), 15, Op.bitwise_and)
    ts(R("m15"), R("im"), 15, Op.bitwise_and)
    tt(R("e8f", p=8), R("ip", p=8), R("mg", p=8), Op.is_equal)
    tt(R("mk1"), R("p15", 0, B), R("m15", 0, B), Op.is_equal)
    cp(R("t0f", p=8), R("tki", p=8))
    ts(R("l0f", p=8), R("lni", p=8), 32.0, Op.mult)
    act(R("mkb"), R("mk1"), Act.Copy, scale=BIG)
    act(R("nid"), R("idb"), Act.Copy, scale=-1.0)
    act(R("idf"), R("idb"), Act.Copy)
    act(R("nse"), R("se0"), Act.Copy, scale=-1.0)
    P1, PQ, PZ, PL, PK, PW, P6, P7 = PSUM
    E8 = R("e8f", p=8)
    mm(R(P1, 0, B), E8, R("t0f", p=8), True, True)
    fill(R("k15"), 15.5)
    mm(R(PQ, 0, B), R("idb"), R("mkb"), True, False)
    mm(R(PQ, 0, B), R("nid"), R("k15"), False, False)
    mm(R(PQ, 0, B), E8, R("t0f", p=8), False, True)
    mm(R(PW, B, 2 * B), R("idb"), R("mkb"), True, False)
    mm(R(PW, B, 2 * B), E8, R("l0f", p=8), False, True)
    fill(R("av"), 1.0)
    fill(R("r8"), 255.0)
    fill(R("r8", 0, 8 * 44, 8), 0.0)
    ts(R("pg"), R("ip"), 4, Op.arith_shift_right)
    tt(R("gb"), R("pg"), R("mg"), Op.is_equal)
    for nm, base in (("elo", 0), ("ehi", 16), ("olo", -1), ("ohi", 15)):
        pick(R(nm), R("gb"), base, -2)
    act(R("gs"), R("gb"), Act.Copy, scale=float(2 ** 16))
    fill(R("rd"), 0.0)
    fill(R("rd", 0, 784, 112), 4096.0)
    fill(R("eq"), 4096.0)
    ts(R("q16"), R("im", 0, 8), 16, Op.mult)
    tt(R("iw"), R("q16"), R("p15", 0, 8), Op.add)

    def lines_of(j):
        a, b = j * C4, (j + 1) * C4
        ts(R("lf", a, b), R("ili", a, b), -15.5, Op.add)

    def lines_act(j):
        a, b = j * C4, (j + 1) * C4
        act(R("lg", a, b), R("lf", a, b), Act.Identity, MAGIC)
        act(R("lt", a, b), R("lg", a, b), Act.Identity, -MAGIC)

    def waits_of(j):
        a, b = j * C4, (j + 1) * C4
        bank = (PW, PL, PZ, PQ)[j]
        mm(R(bank, 0, C4), R("idb"), R("lt", a, b), True, True)
        tt(R("wt", a, b), R("ili", a, b), R(bank, 0, C4), Op.subtract)

    SEG = lambda name, k=0: R(name, k * B + 15, (k + 1) * B, 16)
    S7 = lambda name: R(name, 0, 7)

    def parts_of(n):
        m0, m1 = (0, 3) if n == 6 else (3, 4)
        hi = n + 1
        cp(R("si", 0, 8 * hi, p=B), R("sall", 0, 8 * hi, p=B))
        ts(R("ai", 0, hi), R("av", 0, hi), -1.0, Op.add)
        ts(R("sj", 0, 8 * hi, p=B), R("si", 0, 8 * hi, p=B), 31, Op.bitwise_and)
        ts(R("aj", 0, hi), R("ai", 0, hi), 31, Op.bitwise_and)
        tt(R("pp", 8 * m0, 8 * m1, p=B), R("sj", 8 * m0, 8 * m1, p=B), R("sj", 8 * m0 + 32, 8 * m1 + 32, p=B), Op.add)
        tt(R("af", m0, m1), R("aj", m0, m1), R("aj", m0 + 4, m1 + 4), Op.add)
        if n == 6:
            fill(R("pt"), 0.0)
        for j in range(m0, m1):
            ts(R("pt", 8 * j, 8 * j + 8, p=B), R("pp", 8 * j, 8 * j + 8, p=B), R("af", j, j + 1, p=B), Op.add, 2.0, Op.add)
            if j > 0:
                send(cores[(rank - j) % NR], R("tpa", 8 * j, 8 * j + 8), R("pt", 8 * j, 8 * j + 8), "tp%d" % j)

    def tail_of(n):
        if n < 7:
            act(R("af1"), R(P7, 256, 257), Act.Identity, MAGIC)
            act(R("af2"), R("af1"), Act.Identity, MAGIC, scale=-1.0)
            act(R("av", n + 1, n + 2), R(P7, 256, 257), Act.Identity, R("af2"))
        if n >= 6:
            parts_of(n)

    for n in range(STEPS + 1):
        last = n == STEPS
        y0 = 224 * n
        z, clk = R("yb", y0, y0 + B), R("yb", y0 + B, y0 + 2 * B)
        lns, rot = (None, None) if last else (R("lr", y0, y0 + B), R("lr", y0 + B, y0 + 2 * B))
        if n > 0:
            k = n - 1
            e0 = 224 * k
            ey, ec = R("ey", e0, e0 + B), R("ey", e0 + B, e0 + 2 * B)
            el, et = R("er", e0, e0 + B), R("er", e0 + B, e0 + 2 * B)
            landed("ea%d" % k, prv, [("ey", e0, e0 + (224 if k < 7 else 112))])
            landed("eb%d" % k, prv, [("er", e0, e0 + 224)])
            KM = R(P6, 256, 256 + B)
            mm(KM, R("s15"), el, False, False)
            mm(KM, R("s15"), et, False, True)
            mm(R(PK, 0, B), R("s15"), el, False, False)
            mm(R(PK, 0, B), R("s15"), et, False, True)
            if not last:
                mm(R(P7, B, 2 * B), R("gb"), R("ge2"), True, True)
            for c in (0, B):
                mm(R(PW, c, c + B), R("idb"), R("mkb"), True, False)
                if c:
                    mm(R(PW, c, c + B), R("se1"), el, False, False)
                mm(R(PW, c, c + B), R("nse" if c else "se0"), el, False, True)
            mm(R(PZ, 0, B), R("nid"), ey, True, False)
            if not last:
                mm(R(PQ, 0, B), R("idb"), R("mkb"), True, False)
                mm(R(PQ, 0, B), R("nid"), R("k15"), False, False)
                mm(R(PQ, 0, B), R("idb"), ec, False, False)
                mm(R(P1, 0, B), R("idb"), ec, True, False)
                UC = R(P7, 280, 280 + B)
                PX, PE, PO, PR = R(PW, 256, 256 + B), R(PL, 0, 56), R(PZ, 128, 184), R(P6, 128, 128 + B)
            scan(R("w3", 0, B), R("r3", 0, B), KM, 0.0, Op.min, Op.max)
            tt(S7("nb"), S7("c1"), SEG("w3"), Op.subtract)
            for q in range(7):
                L = 16 * q + 16
                act(R("eq", 112 * q + 112 - L, 112 * q + 112), R(PK, 0, L), Act.Abs, R("nb", q, q + 1))
            ts(S7("dof0"), S7("nb"), -1.0 / 256, Op.mult)
            ts(S7("nk"), S7("nb"), 2.0 ** -20, Op.mult)
            ts(R("wdm"), IND(R("wt"), S7("dof0")), -32.0, Op.add)
            tt(S7("nk"), S7("nk"), S7("iw"), Op.subtract)
            scan(R("em", 0, 448), R("rd", 0, 448), R("eq", 0, 448), 4096.0, Op.max, Op.min)
            scan(R("em", 448, 784), R("rd", 448, 784), R("eq", 448, 784), 4096.0, Op.max, Op.min)
            scan(R("w3", B, 3 * B), R("r3", B, 3 * B), R(PW, 0, 2 * B), 0.0, Op.min, Op.max)
            tt(S7("tp8"), R("em", 111, 784, 112), S7("nk"), Op.add)
            ts(S7("dl"), SEG("w3", 2), -BIG, Op.add)
            ts(S7("lbx"), SEG("w3", 1), -BIG, Op.add)
            tt(S7("mn"), S7("tp8"), S7("cwn"), Op.max)
            ts(S7("doff"), S7("mn"), -4096.0, Op.mult)
            if last:
                mm(R(P6, 0, B), R("se0"), el, True, True)
                mm(R(P6, B, 2 * B), R("se1"), el, True, False)
                mm(R(P6, B, 2 * B), R("nse"), el, False, True)
            if not last:
                act(R("jk"), R(P7, B, 2 * B), Act.Sign, -1.0, R("acc"))
                mm(R(P7, 256, 257), R("on32"), R("q25"), True, False)
                mm(R(P7, 256, 257), R("on32"), R("acc"), False, True)
                if n == 7:
                    tail_of(k)
            landed("zr%d" % k, prv, z[1])
            mm(R(PZ, 0, B), R("idb"), z, False, True)
            if not last:
                mm(R(PQ, 0, B), R("gb"), z, False, False)
                mm(R(P1, 0, B), R("gb"), z, False, True)
                tt(IND(R("wt"), S7("doff")), R("wdm"), z, Op.add)
            act(R("ge"), R(PZ, 0, B), Act.Sign, 0.5)
            mm(R(PQ, 0, B), R("gb" if last else "gs"), R("ge"), last, True)
            if not last:
                mm(UC, R("idb"), ec, True, False)
                mm(UC, R("gb"), z, False, False)
                mm(PX, R("idb"), R("k15"), True, False)
        if last:
            break
        scan(R("qw"), R("r3", 0, B), R(PQ, 0, B), 0.0, Op.min, Op.max)
        if n == 0:
            scan(R("w3", B, 2 * B), R("r3", B, 2 * B), R(PW, B, 2 * B), 0.0, Op.min, Op.max)
            ts(S7("lbx"), SEG("w3", 1), -BIG, Op.add)
        tt(S7("ta"), SEG("qw"), S7("lbx"), Op.add)
        if n > 0:
            ts(S7("sk"), SEG("qw"), BIG + 2.0 ** 16, Op.is_ge)
        ts(S7("mn"), SEG("qw"), MAGIC, Op.add, -MAGIC, Op.add)
        if n > 0:
            ts(S7("qi"), SEG("qw"), 15.5, Op.add)
            tt(S7("sd"), S7("sk"), S7("dl"), Op.mult)
        tt(S7("ta"), S7("ta"), S7("mn"), Op.subtract)
        if n > 0:
            ts(S7("tq"), S7("qi"), 15, Op.bitwise_and)
            tt(S7("ta"), S7("ta"), S7("sd"), Op.add)
            tt(R("ta", 8, 15), S7("tq"), R("lbx", 8, 15), Op.add)
        ts(S7("offs"), S7("ta"), 15.5, Op.add)
        if n > 0:
            cp(R("offs", 8, 15), R("ta", 8, 15))
        act(R("uf"), R(P1, 0, B), Act.Identity, MAGIC)
        act(R("ug"), R("uf"), Act.Identity, -MAGIC)
        if n == 0:
            UC = R(P7, 280, 280 + B)
            mm(UC, E8, R("t0f", p=8), True, False)
        mm(UC, R("nid"), R("ug"), False, True)
        if n > 0:
            act(R("xr"), UC, Act.Copy)
        if n > 0:
            act(R("wf"), IND(R("wt"), S7("offs")), Act.Copy)
            act(lns, IND(R("lt"), S7("offs")), Act.Copy)
            if n < 7:
                tail_of(n - 1)
        if n < 7:
            act(clk, UC, Act.Identity, R("av", n, n + 1))
        if n > 0:
            cp(IND(R("xt"), R("offs", 8, 15)), z)
            lists = ((PO, "olo", "ohi"), (PE, "elo", "ehi"))

            def halves(pb, lo, hi, name, a, start, stop):
                mm(pb, R(lo), R(name, a, a + B, 2), start, False)
                mm(pb, R(hi), R(name, a + 1, a + B, 2), False, stop)
            for pb, lo, hi in lists:
                halves(pb, lo, hi, "xr", 0, True, False)
            mm(PR, R("idb"), R("xr"), True, False)
            mm(PX, R("nid"), R("xr"), False, False)
            mm(PX, R("nid"), R("wf"), False, True)
            ts(R("flx"), PX, MAGIC, Op.add, -MAGIC, Op.add)
            halves(PO, "olo", "ohi", "wf", 0, False, False)
            halves(PO, "olo", "ohi", "lr", y0, False, False)
            halves(PO, "olo", "ohi", "flx", 0, False, True)
            mm(PR, R("idb"), R("wf"), False, False)
            mm(PR, R("idb"), R("flx"), False, True)
            halves(PE, "elo", "ehi", "wf", 0, False, False)
            halves(PE, "elo", "ehi", "lr", y0, False, False)
            halves(PE, "elo", "ehi", "flx", 0, False, True)
            tt(R("rz"), R("wdm"), z, Op.add)
            cp(R("sod"), PO)
            ts(R("ry"), R("rz"), 31, Op.bitwise_and)
            cp(R("sev"), PE)
        else:
            fill(R("wt", W, WT), 0.0)
            fill(R("q25"), 0.25)
            fill(R("on32"), 1.0 / 32)
            cp(R("iob"), R("im", 0, B))
            tt(R("g8"), R("pg", 0, 8), R("im", 0, 8), Op.is_equal)
            ts(S7("c1"), S7("iw"), BIG, Op.add)
            ts(S7("cwn"), S7("iw"), -1.0 / 4096, Op.mult, -W / 4096.0, Op.add)
            ts(R("lbx", 8, 15), S7("iw"), 16.0, Op.mult)
            for j in range(3):
                lines_of(j)
                lines_act(j)
            cp(R("ci"), IND(R("ili"), S7("offs")))
            tt(R("ui"), R("ci"), R(P1, 0, B), Op.add)
            ts(R("cl"), R("ci"), 4064, Op.bitwise_and)
            ts(R("u5"), R("ui"), 31, Op.bitwise_and)
            cp(lns, R("cl"))
            cp(rot, R("u5"))
            for pb, lo, hi, od in ((R(PZ, 128, 184), "olo", "ohi", "sod"), (R(PL, 0, 56), "elo", "ehi", "sev")):
                for o in (0, B):
                    mm(pb, R(lo), R("lr", o, o + B, 2), o == 0, False)
                    mm(pb, R(hi), R("lr", o + 1, o + B, 2), False, o > 0)
                cp(R(od), pb)
            lines_of(3)
            waits_of(0)
        if n > 0:
            act(rot, PR, Act.Copy)
        for a, b in zip(CH, CH[1:]):
            act(R("vo", 8 * a, 8 * b), IND(R("xt"), R("sod", a // 2, b // 2)), Act.Copy)
            if a == 0:
                send(nxt, R("er", y0, y0 + 224), R("lr", y0, y0 + 224), "eb%d" % n)
                ew = 224 if n < 7 else 112
                send(nxt, R("ey", y0, y0 + ew), R("yb", y0, y0 + ew), "ea%d" % n)
        M = CH[-3]
        mm(R(PK, 0, M), R("nid"), R("yb", y0, y0 + M), True, False)
        mm(R(P6, 0, B - M), R("nid"), R("yb", y0 + M, y0 + B), True, False)

        def least(k):
            a, b = CH[k], CH[k + 1]
            tt(R("mn2", 8 * a, 8 * b), IND(R("xt"), R("sev", a // 2, b // 2)), R("vo", 8 * a, 8 * b), Op.min)

        def greatest(a, b):
            scan(R("mx", 8 * a, 8 * b), R("r8", 0, 8 * (b - a)), R("mn2", 8 * a, 8 * b), 0.0, Op.min, Op.max)
        for k in range(len(CH) - 1):
            least(k)
            if k > 0:
                greatest(CH[k - 1], CH[k])
        greatest(CH[-2], B)
        zo = B * n
        mm(R(PK, 0, M), R("idb"), R("mx", 7, 8 * M, 8), False, True)
        mm(R(P6, 0, B - M), R("idb"), R("mx", 8 * M + 7, 8 * B, 8), False, True)
        act(R("zo", zo, zo + M), R(PK, 0, M), Act.Abs)
        act(R("zo", zo + M, zo + B), R(P6, 0, B - M), Act.Abs)
        zo = R("zo", zo, zo + B)
        send(nxt, R("yb", y0 + 224, y0 + 224 + B), zo, "zr%d" % n)
        if n > 0:
            cp(IND(R("wt"), S7("doff")), R("ry"))
        KM = R(P6, 256, 256 + B)
        mm(KM, R("idb"), R("mkb"), True, False)
        mm(KM, R("idb"), R("iob"), False, False)
        mm(R(PK, 0, B), R("idb"), R("iob"), True, False)
        if n == 0:
            lines_act(3)
            for j in range(1, 4):
                waits_of(j)
        if n < 7:
            mm(R(P7, 0, B), R("nid"), z, True, False)
            mm(R(P7, 0, B), R("idb"), zo, False, True)
            act(R("ge2"), R(P7, 0, B), Act.Sign, 0.5)
        mm(R(PL, 264, 272, p=B), zo, R("g8"), True, True)
        act(R("sall", 8 * n, 8 * n + 8, p=B), R(PL, 264, 272, p=B), Act.Copy)
        if n == 7:
            tail_of(n)

    tt(R("rz"), R("wdm"), z, Op.add)
    ts(R("ry"), R("rz"), 31, Op.bitwise_and)
    cp(IND(R("wt"), S7("doff")), R("ry"))
    dma("Y", T.yw[:, :], T.wt[:, 0:W], [("wt", 0, W)], [])
    dma("S", T.yy[:, :], T.yb[:, y0:y0 + B], z[1], [])
    ts(R("fs"), R(PQ, 0, B), 1.0, Op.is_ge)
    tt(R("fd"), R("fs"), R(P6, B, 2 * B), Op.mult)
    tt(R("fl"), R("fd"), R(P6, 0, B), Op.add)
    ts(R("fy"), R("fl"), 1.0 / 32, Op.mult)
    dma("S", T.yl[:, :], T.fy[0:128:16, :], [("fy", 0, B)], [])
    for j in range(1, 4):
        landed("tp%d" % j, cores[(rank + j) % NR], [("tpa", 8 * j, 8 * j + 8)])
    idq = (T.idf[0:B, 0:B], [("idf", 0, B)], [])
    for j in range(4):
        mm(R(P1, 0, B, p=8), R("pt" if j == 0 else "tpa", 8 * j, 8 * j + 8, p=B), idq, j == 0, j == 3)
    tt(R("ft", p=8), R("tki", p=8), R(P1, 0, B, p=8), Op.add)
    ts(R("fu", p=8), R("ft", p=8), 4095, Op.bitwise_and)
    cp(R("fv", p=8), R("fu", p=8))
    dma("Y", T.yt[:, :], T.fv[0:8, :], [("fv", 0, B)], [])
    for q in ("V", "S", "P", "G"):
        g.wait_ge(T.sem[sems[q]], cnt[q])
    for name in dma_all:
        g.wait_ge(T.sem[name], 16)
    g.wait_ge(T.sem.lsem, sent[0])
